import numpy as np, ml_dtypes
CORES = [16,17,18,19,32,33,34,35]
N = 8
BF = ml_dtypes.bfloat16
def gentries(a):
    return np.ascontiguousarray(a.reshape(8, 16, -1).transpose(0, 2, 1)).reshape(8, -1)
def gtable(e):
    e = np.asarray(e); return np.ascontiguousarray(e.reshape(8, -1, 16).transpose(0, 2, 1)).reshape(128, -1).astype(np.int32)
DR, NZ, Z, R = 1, 4, 2048, 2
ND, DD, C = N * DR, N * DR - 2, 2 * Z // R
def disks(x):
    return np.ascontiguousarray(x.astype(np.float32).astype(np.int32).reshape(N, 128, DR, NZ, Z).transpose(0, 2, 3, 1, 4)).reshape(ND, NZ, 128, Z)
def turns(pi):
    return np.ascontiguousarray(np.stack([gentries(a) for a in pi]).reshape(N, 8, DR, NZ, Z).transpose(0, 2, 3, 1, 4)).reshape(ND, NZ, 8, Z)
def follow(pa, pb):
    inv = np.zeros(Z, np.int64); inv[pb] = np.arange(Z)
    return inv, pa[inv]
def solve(w, p, a, b, ze):
    ps = w[DD].copy(); qs = w[DD + 1].copy()
    for i in range(DD):
        if i != a and i != b: ps -= w[i]; qs -= w[i][:, p[i]]
    ps = np.ascontiguousarray(ps.T) & 255; qs = np.ascontiguousarray(qs.T) & 255
    inv, nx = follow(p[a], p[b]); d = ps - qs[inv]; live = (ze == 0)[:, None]; xa = np.zeros((Z, 16), np.int32)
    for s in range(128): xa = np.where(live, d + xa[nx], 0) & 255
    return xa, (ps - xa) & 255, qs
def some_bytes(rng, *shape):
    return rng.integers(0, 256, shape, dtype=np.uint8).astype(np.int32)
def some_turns(rng):
    return rng.permuted(np.tile(np.arange(Z), (DD, NZ, 8, 1)), axis=-1)
def some_pairs(rng):
    o = rng.permutation(DD); return np.array([[o[g % DD], o[(g + rng.integers(1, DD)) % DD]] for g in range(8)])
def marks(rng, nx, gaps, first):
    m = np.zeros(Z, bool); n = nx.tolist(); seen = [False] * Z; u = 0
    for s in first + rng.permutation(Z).tolist():
        left = 0
        while not seen[s]:
            seen[s] = True
            if left == 0: m[s] = True; left = gaps[u]; u += 1
            left -= 1; s = n[s]
    return m
def write(rng, v, p, lo, far=False, first=None):
    ze = np.zeros((NZ, 8, Z), bool); qs = np.zeros((NZ, 128, Z), np.int32)
    for z in range(NZ):
        for g in range(8):
            a, b = lo[g]; k = slice(16 * g, 16 * g + 16)
            gaps = np.where(rng.random(Z) < (1 if far else 0.25), 128, rng.integers(1, 129, Z)).tolist()
            ze[z, g] = marks(rng, follow(p[a, z, g], p[b, z, g])[1], gaps, [] if first is None else first[g])
            v[a, z, k] *= ~ze[z, g]
            for i in range(DD): qs[z, k] += v[i, z, k][:, p[i, z, g]]
    ps = np.add.reduce(v, axis=0)
    for g in range(8):
        for i in lo[g]: v[i, :, 16 * g:16 * g + 16] = some_bytes(rng, NZ, 16, Z)
    w = np.concatenate([v, ps[None] & 255, qs[None] & 255]); t = np.concatenate([p, np.tile(np.arange(Z), (2, NZ, 8, 1))])
    t = t.reshape(N, DR, NZ, 8, Z).transpose(0, 3, 1, 2, 4).reshape(N, 8, -1)
    return {"x": np.ascontiguousarray(w.reshape(N, DR, NZ, 128, Z).transpose(0, 3, 1, 2, 4)).reshape(N, 128, -1).astype(np.float32).astype(BF),
            "pi": np.stack([gtable(e) for e in t]), "lost": np.stack([np.repeat(lo, 16, axis=0).astype(np.int32)] * N), "zero": np.stack([gtable(ze[q // R]) for q in range(N)])}
def setup_inputs(rng):
    return write(rng, some_bytes(rng, DD, NZ, 128, Z), some_turns(rng), some_pairs(rng))
def setup_inputs_long(rng):
    p = some_turns(rng); lo = some_pairs(rng)
    for z in range(NZ):
        for g in range(8):
            o = np.arange(Z) if g == 0 else np.arange(Z)[::-1] if g == 1 else rng.permutation(Z)
            c = np.zeros(Z, np.int64); c[o] = np.roll(o, -1); a, b = lo[g]; p[a, z, g] = c[p[b, z, g]]
    return write(rng, some_bytes(rng, DD, NZ, 128, Z), p, lo, True, [[0], [Z - 1]] + [[]] * 6)
def setup_inputs_short(rng):
    p = some_turns(rng); lo = some_pairs(rng); h = rng.permutation(8)
    for z in range(NZ):
        for u in range(6):
            g = h[u]; a, b = lo[g]; o = rng.permutation(Z); c = np.arange(Z)
            if u == 1: c[o[0::2]] = o[1::2]; c[o[1::2]] = o[0::2]
            if u == 2:
                i = 0
                while i < Z:
                    n = int(rng.integers(1, 6)); k = o[i:i + n]; c[k] = np.roll(k, -1); i += n
            if u < 3: p[a, z, g] = c[p[b, z, g]]
            if u == 3:
                for i in range(DD):
                    if i != a and i != b: p[i, z, g] = np.arange(Z)
            if u == 4: p[b, z, g] = np.arange(Z)
            if u == 5: p[a, z, g] = np.arange(Z)
    return write(rng, some_bytes(rng, DD, NZ, 128, Z), p, lo, True)
def setup_inputs_pair(rng):
    lo = np.array([[0, DD - 1] if e else [DD - 1, 0] for e in rng.permutation(8) < 4])
    return write(rng, some_bytes(rng, DD, NZ, 128, Z), some_turns(rng), lo)
def setup_inputs_spread(rng):
    v = some_bytes(rng, DD, NZ, 128, Z) & rng.choice(np.array([0, 1, 3, 15, 63, 128, 255], np.int32), (DD, NZ, 1, Z))
    v[rng.random(v.shape, dtype=np.float32) < 0.2] = 255
    return write(rng, v, some_turns(rng), some_pairs(rng))
def check_inputs(d):
    bad = []; x = d["x"].astype(np.float32); p = turns(d["pi"]); lo = d["lost"]; ze = d["zero"]
    if not ((x >= 0) & (x <= 255) & (x == np.floor(x))).all(): bad.append("bytes")
    if not (np.sort(p, axis=-1) == np.arange(Z)).all(): bad.append("permutations")
    if not (p[DD:] == np.arange(Z)).all(): bad.append("identity")
    if not ((lo >= 0) & (lo < DD)).all() or not (lo[:, :, 0] != lo[:, :, 1]).all() or not (lo == np.repeat(lo[0, ::16], 16, axis=0)).all(): bad.append("lost")
    if not ((ze == 0) | (ze == 1)).all() or not all((ze[q] == ze[q - q % R]).all() for q in range(N)): bad.append("zero")
    if bad: return bad
    v = disks(d["x"])
    for z in range(NZ):
        e = gentries(ze[z * R])
        for g in range(8):
            a, b = int(lo[0, 16 * g, 0]), int(lo[0, 16 * g, 1]); nx = follow(p[a, z, g], p[b, z, g])[1]; m = e[g][nx] == 1; first = m
            for s in range(127): m = first | m[nx]
            if not m.all(): bad.append("chains")
            xa, xb, qs = solve(v[:, z, 16 * g:16 * g + 16], p[:, z, g], a, b, e[g])
            if not (((xa[p[a, z, g]] + xb[p[b, z, g]]) & 255) == qs).all(): bad.append("sums")
    return sorted(set(bad))
def reference(x, pi, lost, zero):
    v = disks(x); p = turns(pi); y = np.zeros((N, 128, C), np.float32)
    for z in range(NZ):
        e = gentries(zero[z * R])
        for g in range(8):
            xa, xb, qs = solve(v[:, z, 16 * g:16 * g + 16], p[:, z, g], int(lost[0, 16 * g, 0]), int(lost[0, 16 * g, 1]), e[g])
            both = np.concatenate([xa, xb]).T
            for s in range(R): y[z * R + s, 16 * g:16 * g + 16] = both[:, s * C:(s + 1) * C]
    return {"y": y.astype(BF)}

@@ -1,0 +1,508 @@
+from concourse.bass import DstId, RemoteDMATransfer
+from concourse.mybir import AluOpType, ActivationFunctionType
+
+OP = AluOpType
+COPY = ActivationFunctionType.Copy
+IDENT = ActivationFunctionType.Identity
+Z = 2048
+H = 1024
+WZ = Z + 256
+NL = 90
+LISTS = ["lb", "li"] + ["nl%d" % t for t in range(7)]
+CH = ((1024, 2048), (0, 512), (512, 1024))
+
+SCRATCH = {"ps": ("psum", [128, 4096], "float32")}
+for _names, _cols, _dt in (
+        ("xs qs", 4 * Z, "bfloat16"), ("lfp lfq lnp", 4 * H, "bfloat16"), ("lnq", 4 * Z, "bfloat16"),
+        ("zm yo dd iot inv invz", Z, "bfloat16"),
+        ("dm dp", 512, "bfloat16"), ("zeb bm bz base idb idn", 128, "bfloat16"), ("na nb", WZ, "bfloat16"), ("il", 256, "bfloat16"),
+        ("pin", 512, "int32"), ("losti", 2, "int32"), ("zin i1 i3", 128, "int32"), ("i2 i2b", 16, "int32"),
+        ("i4 i4b i4c", 4, "int32"), ("i5", 8, "int32"), ("v7 fi", WZ, "int32"), ("fj", Z, "int32"),
+        ("lp", 512, "uint16"), (" ".join(LISTS) + " la", 128, "uint16"),
+        ("ph", 512, "float16"), ("lpi sa sb", 768, "float16"), ("idh", 128, "float16"),
+        ("rfp rfq", Z, "float16"), ("fsp fsq relay", H, "float16"), ("nsp rnp", H, "float32"),
+        ("lostf", 2, "float32"), ("kcol odd even wcol", 4, "float32"), ("rmask", 16, "float32"), ("ea eb ms mn mp bev", 8, "float32"),
+        ("p1 q1 vc", Z, "float32"), ("wa wb", WZ, "float32")):
+    for _n in _names.split():
+        SCRATCH[_n] = ("sbuf", [128, _cols], _dt)
+SEMAPHORES = (["l%d" % i for i in range(NL)] + ["snt", "rpi", "rrelay"]
+              + ["r%s%d" % (b, s) for b in ("lfp", "lfq", "lnp", "lnq") for s in range(4)]
+              + ["rrfp0", "rrfp1", "rrfq0", "rrfq1", "rrnp", "rv0", "rv1", "rv2"] + ["r" + n for n in LISTS])
+
+
+def tracker(g, T):
+    E = {"g": g, "v": g.vector, "s": g.scalar, "t": g.tensor, "y": g.sync}
+    known = {e: {} for e in E}
+    count, waited, recs = {}, {}, {}
+    free = ["l%d" % i for i in range(NL)]
+    own = {e: [] for e in E}
+
+    def wait(e, tok):
+        sem, val, snap = tok
+        k = known[e]
+        if k.get(sem, 0) >= val:
+            return
+        E[e].wait_ge(T.sem[sem], val)
+        waited[sem] = max(waited.get(sem, 0), val)
+        k[sem] = val
+        for s, n in snap.items():
+            if k.get(s, 0) < n:
+                k[s] = n
+
+    def span(r):
+        b, a, z = r
+        return (b, a // 512 * 512, -(-z // 512) * 512) if b == "ps" else (b, a, z)
+
+    def conflicts(who, reads, writes, acc):
+        out = []
+        for r in reads:
+            b, a, z = span(r)
+            for (x, y, kind, w, tok) in recs.get(b, []):
+                if x < z and a < y and (kind == "w" or (b == "ps" and w != who)):
+                    out.append(tok)
+        for r in writes:
+            b, a, z = span(r)
+            for (x, y, kind, w, tok) in recs.get(b, []):
+                if x < z and a < y and not (w == who and (kind == "r" or acc)):
+                    out.append(tok)
+        return out
+
+    def note(reads, writes, who, tok):
+        for r in writes:
+            b, a, z = span(r)
+            recs[b] = [q for q in recs.get(b, []) if not (a <= q[0] and q[1] <= z and q[4] is not tok)] + [(a, z, "w", who, tok)]
+        for r in reads:
+            b, a, z = span(r)
+            recs.setdefault(b, []).append((a, z, "r", who, tok))
+
+    def batch(e, items, dma=False, acc=False):
+        who = "dma" if dma else e
+        ins = []
+        for fn, reads, writes in items:
+            for t in sorted(conflicts(who, reads, writes, acc), key=lambda t: -len(t[2])):
+                wait(e, t)
+            ins.append(fn())
+        done = [s for s in own[e] if known[e].get(s, 0) == count[s]]
+        if not done:
+            done = [free.pop(0)]
+            own[e].append(done[0])
+            count[done[0]] = 0
+        sem = done[0]
+        for i in ins:
+            i.then_inc(T.sem[sem], 16 if dma else 1)
+            count[sem] += 16 if dma else 1
+        tok = (sem, count[sem], dict(known[e]))
+        for fn, reads, writes in items:
+            note(reads, writes, who, tok)
+
+    def op(e, fn, reads, writes, dma=False):
+        batch(e, [(fn, reads, writes)], dma)
+
+    def landing(b, a, z, sem, val):
+        count[sem] = val
+        note([], [(b, a, z)], "remote", (sem, val, {}))
+
+    def reading(e, reads):
+        for t in conflicts(e, reads, [], False):
+            wait(e, t)
+
+    def finish(sent):
+        count["snt"] = sent
+        for s, n in count.items():
+            if waited.get(s, 0) < n:
+                g.wait_ge(T.sem[s], n)
+
+    return op, batch, landing, reading, finish
+
+
+def bits(es):
+    return sum(1 << e for e in es)
+
+
+def relay_of(core, T, topo):
+    cs = topo.cores_of(core)
+    same = [c for c in cs if T.rank_of(c) is not None and topo.die(c) == topo.die(core)]
+    free = [c for c in cs if T.rank_of(c) is None and topo.die(c) != topo.die(core)]
+    return free[same.index(core)]
+
+
+def rank_program(g, core, T, topo):
+    rank = T.rank_of(core)
+    C = list(T.cores)
+    if rank is None:
+        for c in C[0::2]:
+            if topo.chip(c) == topo.chip(core) and relay_of(c, T, topo) == core:
+                here = [d for d in C if topo.chip(d) == topo.chip(c)]
+                zs = [z for z in range(4) if C[2 * z] not in here]
+                to = C[2 * zs[here.index(c) // 2] + 1]
+                a = topo.addr(to)
+                g.wait_ge(T.sem["rrelay"], len(topo.engines(c, to)))
+                g.remote_dma(out_ap=T.rfp[:, 0:H], in_ap=T.relay[:], remote_sem=T.sem["rrfp0"],
+                             local_sem=T.sem["snt"], pid=a[1], routing_id=a[0], dma_engine_mask=topo.mask(core, to))
+                g.wait_ge(T.sem["snt"], len(topo.engines(core, to)))
+        return
+    V, S, PE = g.vector, g.scalar, g.tensor
+    op, batch, landing, reading, finish = tracker(g, T)
+    local = [r for r in range(8) if topo.chip(C[r]) == topo.chip(core)]
+    l = local.index(rank)
+    near = sorted({r // 2 for r in local})
+    far = [z for z in range(4) if z not in near]
+    isA = rank % 2 == 0
+    zone = rank // 2
+    data = rank < 6
+    hasP = [s for s in range(4) if local[s] != 7]
+    hasQ = [s for s in range(4) if local[s] != 6]
+    others = [d for d in range(4) if d != l]
+    away = [r for r in range(8) if r not in local]
+    all_es = topo.engines(core, C[local[others[0]]])
+    off_es = topo.engines(core, C[away[0]])
+    on_es = [e for e in all_es if e not in off_es]
+    sent = [0]
+
+    def R(b, a=0, z=None):
+        return (b, a, SCRATCH[b][1][1] if z is None else z)
+
+    def send(to, sem, dst, src, reads, es=None):
+        reading("g", reads)
+        a = topo.addr(to)
+        es = topo.engines(core, to) if es is None else es
+        g.remote_dma(out_ap=dst, in_ap=src, remote_sem=T.sem[sem], local_sem=T.sem["snt"], pid=a[1], routing_id=a[0],
+                     dma_engine_mask=bits(es))
+        sent[0] += len(es)
+
+    def send_all(parts, reads):
+        reading("g", reads)
+        trs = []
+        for r, sem, dst, src, es in parts:
+            a = topo.addr(C[r])
+            trs.append(RemoteDMATransfer(dst_ids=[DstId(rid=a[0], pnc=a[1])], dma_engine_mask=bits(es),
+                                         remote_sem=T.sem[sem], src=src, dst=dst))
+            sent[0] += len(es)
+        g.remote_dma_fused(trs, local_sem=T.sem["snt"])
+
+    def width(r):
+        return len(topo.engines(C[r], core))
+    for b, who, w, n in (("lfp", hasP, H, 4), ("lfq", hasQ, H, 4), ("lnp", hasP, H, len(on_es)), ("lnq", hasQ, Z, len(all_es))):
+        for s in who:
+            if s != l and not (isA and b == "lnq"):
+                landing(b, s * w, (s + 1) * w, "r%s%d" % (b, s), n)
+    if isA:
+        landing("lpi", 0, 768, "rpi", 4 * (5 if data else 6))
+        for c, (c0, c1) in enumerate(CH):
+            landing("v7", c0, c1, "rv%d" % c, width(rank + 1))
+    else:
+        for n in LISTS:
+            landing(n, 0, 128, "r" + n, width(rank - 1))
+        landing("rnp", 0, H, "rrnp", width(rank - 1))
+        for b in ("rfp", "rfq"):
+            for h in range(2):
+                landing(b, h * H, (h + 1) * H, "r%s%d" % (b, h), width(away[0]))
+
+    def load(e, dst, src, w):
+        q = g.sync if e == "y" else S
+        op(e, lambda: q.dma_start(dst, src), [], [w], True)
+
+    def loadx(e, z):
+        load(e, T.xs[:, z * Z:(z + 1) * Z], T.x[:, z * Z:(z + 1) * Z], R("xs", z * Z, (z + 1) * Z))
+    mine_first = sorted(near, key=lambda z: z != zone)
+    if data:
+        load("y", T.pin[:], T.pi[:], R("pin"))
+    load("s", T.losti[:], T.lost[:], R("losti"))
+    if isA:
+        load("s", T.zin[:], T.zero[:], R("zin"))
+    loadx("y", far[0])
+    loadx("s", far[1])
+    for z in mine_first:
+        loadx("y", z)
+
+    def iota(b, pattern, base, cm, **kw):
+        op("g", lambda: g.iota(T[b][:], pattern, base, cm, **kw), [], [R(b)])
+    iota("i1", [[-1, 128]], 0, 1)
+    iota("i5", [[1, 8]], 0, 0)
+    if isA:
+        iota("i2", [[-1, 16]], 16, 1)
+        iota("i3", [[1, 8], [0, 16]], 0, 0)
+        iota("i4", [[0, 4]], 0, 1)
+        iota("il", [[1, 256]], 0, 0, allow_small_or_imprecise_dtypes=True)
+
+    def ts(out, in0, s1, s2, op0, op1, reads, writes):
+        a = (out, in0, s1, s2, op0) if op1 is None else (out, in0, s1, s2, op0, op1)
+        op("v", lambda: V.tensor_scalar(*a), reads, writes)
+
+    def tt(out, in0, in1, o, reads, writes):
+        op("v", lambda: V.tensor_tensor(out, in0, in1, o), reads, writes)
+
+    def cp(out, in_, reads, writes):
+        op("v", lambda: V.tensor_copy(out, in_), reads, writes)
+
+    def fill(b, c, a=Z, z=WZ):
+        op("v", lambda: V.memset(T[b][:, a:z], c), [], [(b, a, z)])
+
+    def scaled(n, dst, idn, col):
+        items = []
+        for i in range(n):
+            b, j = col(i)
+            items.append((lambda i=i, b=b, j=j: V.tensor_scalar(T[dst][:, i * 128:(i + 1) * 128], T[idn][:], T[b][:, j:j + 1], None, OP.mult),
+                          [R(idn), R(b)], [R(dst, i * 128, (i + 1) * 128)]))
+        batch("v", items)
+
+    if isA:
+        fill("dd", 0.0, 0, Z)
+    ts(T.idb[:], T.i1[:], 0, None, OP.is_equal, None, [R("i1")], [R("idb")])
+    if isA:
+        ts(T.idh[:], T.i1[:], 0, None, OP.is_equal, None, [R("i1")], [R("idh")])
+        ts(T.i2b[:], T.i2[:], 15, None, OP.bitwise_and, None, [R("i2")], [R("i2b")])
+        ts(T.i4b[:], T.i4[:], 4, None, OP.arith_shift_right, None, [R("i4")], [R("i4b")])
+        ts(T.i4c[:], T.i4[:], 1, None, OP.bitwise_and, None, [R("i4")], [R("i4c")])
+        ts(T.rmask[:], T.i2b[:], 0, None, OP.is_equal, None, [R("i2b")], [R("rmask")])
+        cp(T.kcol[:], T.i4b[:], [R("i4b")], [R("kcol")])
+        cp(T.odd[:], T.i4c[:], [R("i4c")], [R("odd")])
+    if data:
+        cp(T.ph[:], T.pin[:], [R("pin")], [R("ph")])
+        where = [(2 * z, off_es[4 * i:4 * i + 4]) for i, z in enumerate(far)]
+        where += [(r, on_es[4 * i:4 * i + 4]) for i, r in enumerate(2 * z for z in near if 2 * z != rank)]
+        send_all([(r, "rpi", T.lpi[:, rank * 128:(rank + 1) * 128], T.ph[:, (r // 2) * 128:(r // 2 + 1) * 128], es)
+                  for r, es in where], [R("ph")])
+        cp(T.lp[:], T.pin[:], [R("pin")], [R("lp")])
+    cp(T.lostf[:], T.losti[:], [R("losti")], [R("lostf")])
+    ts(T.ea[:], T.i5[:], T.lostf[:, 0:1], None, OP.is_equal, None, [R("i5"), R("lostf")], [R("ea")])
+    ts(T.eb[:], T.i5[:], T.lostf[:, 1:2], None, OP.is_equal, None, [R("i5"), R("lostf")], [R("eb")])
+    tt(T.ms[:], T.ea[:], T.eb[:], OP.add, [R("ea"), R("eb")], [R("ms")])
+    ts(T.mn[:], T.ms[:], -1.0, None, OP.add, None, [R("ms")], [R("mn")])
+    nd = len([r for r in local if r < 6])
+    scaled(nd, "dm", "idb", lambda i: ("mn", local[i]))
+
+    def weight(s, plus):
+        m, i = ("dm", "idb") if plus else ("dp", "idn")
+        return (T[m][:, s * 128:(s + 1) * 128], R(m, s * 128, (s + 1) * 128)) if local[s] < 6 else (T[i][:], R(i))
+
+    def pick(e, dst, d0, src, s0, s1, lst, t0, n):
+        out, in_ = T[dst][:, d0:d0 + n], T[src][:, s0:s1].indirect(T[lst][:, t0:t0 + n // 16])
+        rd, wr = [R(src, s0, s1), R(lst, t0, t0 + n // 16)], [R(dst, d0, d0 + n)]
+        if e == "v":
+            op("v", lambda: V.tensor_copy(out, in_), rd, wr)
+        else:
+            op("s", lambda: S.activation(out, in_, COPY), rd, wr)
+
+    def gather(e, z):
+        pick(e, "qs", z * Z, "xs", z * Z, (z + 1) * Z, "lp", z * 128, Z)
+
+    def piece(zs, srcb, landb, d, w, es):
+        a = zs[d // 2] * Z + (d % 2 * H if w == H else 0)
+        return (local[d], "r%s%d" % (landb, l), T[landb][:, l * w:(l + 1) * w], T[srcb][:, a:a + w], es), R(srcb, a, a + w)
+
+    def far_pieces(srcb, landb):
+        ps = [piece(far, srcb, landb, d, H, topo.engines(core, C[local[d]])[4 * i:4 * i + 4]) for i, d in enumerate(others)]
+        send_all([p[0] for p in ps], [p[1] for p in ps])
+
+    def near_pieces(srcb, landb, to, w, es):
+        for d in sorted(to, key=lambda d: d // 2 != l // 2):
+            (r, sem, dst, src, es), rd = piece(near, srcb, landb, d, w, es)
+            send(C[r], sem, dst, src, [rd], es)
+
+    qsrc = "qs" if data else "xs"
+    if data:
+        gather("v", far[0])
+        gather("s", far[1])
+    if l in hasP:
+        far_pieces("xs", "lfp")
+    if l in hasQ:
+        far_pieces(qsrc, "lfq")
+    if l in hasP:
+        near_pieces("xs", "lnp", others, H, on_es)
+    if not isA:
+        ts(T.mp[:], T.mn[:], -1.0, None, OP.mult, None, [R("mn")], [R("mp")])
+        scaled(nd, "dp", "idb", lambda i: ("mp", local[i]))
+        ts(T.idn[:], T.idb[:], -1.0, None, OP.mult, None, [R("idb")], [R("idn")])
+    if data:
+        gather("s", mine_first[0])
+        gather("s" if isA else "v", mine_first[1])
+
+    def addup(zs, srcb, landb, who, bank, mine, half=None, plus=True):
+        items = []
+        z, w, d, h = (zs[l // 2], H, 0, l % 2) if half is None else (zone, Z, half * H, half)
+        seq = [s for s in who if s == l] + [s for s in who if s != l]
+        for n, s in enumerate(seq):
+            if (s == l) != mine:
+                continue
+            wt, wr = weight(s, plus)
+            for b in range(2):
+                buf, a = (srcb, z * Z + h * H + 512 * b) if s == l else (landb, s * w + d + 512 * b)
+                o = (bank + b) * 512
+                items.append((lambda o=o, wt=wt, buf=buf, a=a, st=n == 0, en=n == len(seq) - 1:
+                              PE.matmul(T.ps[:, o:o + 512], wt, T[buf][:, a:a + 512], st, en),
+                              [wr, R(buf, a, a + 512)], [R("ps", o, o + 512)]))
+        if items:
+            batch("t", items, acc=True)
+
+    def evac(dst, bank):
+        for b in range(2):
+            o = (bank + b) * 512
+            ts(T[dst][:, b * 512:b * 512 + 512], T.ps[:, o:o + 512], 1.0, None, OP.add, None, [R("ps", o, o + 512)], [R(dst, b * 512, b * 512 + 512)])
+
+    def far_send(src, dst):
+        h = l % 2
+        send(C[2 * far[l // 2] + 1], "r%s%d" % (dst, h), T[dst][:, h * H:(h + 1) * H], T[src][:], [R(src)])
+
+    def far_p():
+        evac("fsp", 0)
+        if isA:
+            send(relay_of(core, T, topo), "rrelay", T.relay[:], T.fsp[:], [R("fsp")], off_es)
+        else:
+            far_send("fsp", "rfp")
+
+    def far_q():
+        evac("fsq", 2)
+        far_send("fsq", "rfq")
+
+    def store(c0, c1):
+        op("y", lambda: g.sync.dma_start(T.y[:, c0:c1], T.yo[:, c0:c1]), [R("yo", c0, c1)], [], True)
+
+    FP, FQ = (far, "xs", "lfp", hasP, 0), (far, qsrc, "lfq", hasQ, 2)
+    NP = (near, "xs", "lnp", hasP, 4)
+    solvers = [d for d in others if d % 2 == 1]
+    if isA:
+        B = C[rank + 1]
+        cp(T.zeb[:], T.zin[:], [R("zin")], [R("zeb")])
+        scaled(6, "sb", "idh", lambda i: ("eb", i))
+        scaled(6, "sa", "idh", lambda i: ("ea", i))
+        ts(T.even[:], T.i4c[:], 0, None, OP.is_equal, None, [R("i4c")], [R("even")])
+        ts(T.bm[:], T.i3[:], T.kcol[:, 0:1], None, OP.is_equal, None, [R("i3"), R("kcol")], [R("bm")])
+        ts(T.wcol[:, 0:1], T.rmask[:, 0:1], 256.0, T.rmask[:, 1:2], OP.mult, OP.add, [R("rmask")], [R("wcol")])
+        ts(T.bev[:], T.i5[:], T.even[:, 0:1], None, OP.mult, None, [R("i5"), R("even")], [R("bev")])
+        ts(T.base[:], T.bm[:], T.wcol[:, 0:1], None, OP.mult, None, [R("bm"), R("wcol")], [R("base")])
+        batch("v", [(lambda b=b: V.tensor_scalar(T.iot[:, b * 256:(b + 1) * 256], T.il[:], T.odd[:, 0:1], T.bev[:, b:b + 1], OP.mult, OP.add),
+                     [R("il"), R("odd"), R("bev")], [R("iot", b * 256, (b + 1) * 256)]) for b in range(8)])
+        batch("s", [(lambda p=p: S.activation(T.zm[:, p:Z:16], T.zeb[:], COPY, scale=T.rmask[:, p:p + 1]),
+                     [R("zeb"), R("rmask")], [R("zm")]) for p in range(16)], acc=True)
+        batch("s", [(lambda r=r: S.activation(T.dd[:, r * 128 + r:(r + 1) * 128:16], T.base[:, r:128:16], COPY),
+                     [R("base")], [R("dd")]) for r in range(16)], acc=True)
+        for nm in ("na", "nb"):
+            op("s", lambda: S.activation(T[nm][:, Z:WZ], T.il[:], IDENT, scale=0.0, bias=8.0), [R("il")], [R(nm, Z, WZ)])
+        addup(*FP, True)
+        addup(*FQ, True)
+        for nm, dst, o in (("sb", "lb", 2048), ("sa", "la", 2560)):
+            items = []
+            for i in range(6):
+                buf, a = ("ph", zone * 128) if i == rank else ("lpi", i * 128)
+                items.append((lambda i=i, buf=buf, a=a: PE.matmul(T.ps[:, o:o + 128], T[nm][:, i * 128:(i + 1) * 128], T[buf][:, a:a + 128], i == 0, i == 5),
+                              [R(nm, i * 128, (i + 1) * 128), R(buf, a, a + 128)], [R("ps", o, o + 128)]))
+            batch("t", items, acc=True)
+            cp(T[dst][:], T.ps[:, o:o + 128], [R("ps", o, o + 128)], [R(dst)])
+        send(B, "rlb", T.lb[:], T.lb[:], [R("lb")])
+        if l in hasQ:
+            near_pieces(qsrc, "lnq", solvers, Z, all_es)
+        addup(*FP, False)
+        addup(*NP, True)
+        addup(*FQ, False)
+
+        def scat(i):
+            cp(T.inv[:, 0:Z].indirect(T.lb[:, i * 32:(i + 1) * 32]), T.iot[:, i * 512:(i + 1) * 512], [R("lb"), R("iot")], [R("inv")])
+        scat(0)
+        far_p()
+        scat(1)
+        scat(2)
+        far_q()
+        fill("bz", 0.0, 0, 128)
+        ts(T.bz[:, 0:128:2], T.bm[:, 0:128:2], 8.0, None, OP.mult, None, [R("bm")], [R("bz")])
+        fill("fi", 255)
+        scat(3)
+        addup(*NP, False)
+        for b in range(2):
+            o, c0 = 2048 + 512 * b, 512 * b
+            op("s", lambda: S.activation(T.nsp[:, c0:c0 + 512], T.ps[:, o:o + 512], COPY, scale=-1.0), [R("ps", o, o + 512)], [R("nsp", c0, c0 + 512)])
+        send(B, "rrnp", T.rnp[:], T.nsp[:], [R("nsp")])
+        for b in range(4):
+            c0, c1 = 512 * b, 512 * b + 512
+            op("t", lambda: PE.matmul(T.ps[:, c0:c1], T.bz[:], T.zm[:, c0:c1], True, True), [R("bz"), R("zm", c0, c1)], [R("ps", c0, c1)])
+            tt(T.invz[:, c0:c1], T.inv[:, c0:c1], T.ps[:, c0:c1], OP.max, [R("inv", c0, c1), R("ps", c0, c1)], [R("invz", c0, c1)])
+
+        def rows(src, h):
+            c0, c1, o = h * H, (h + 1) * H, 2048 + 512 * h
+            batch("t", [(lambda r=r: PE.matmul(T.ps[:, o:o + 64], T.dd[:, r * 128:(r + 1) * 128], T[src][:, c0 + r:c1:16], r == 0, r == 15),
+                         [R("dd"), R(src, c0, c1)], [R("ps", o, o + 64)]) for r in range(16)], acc=True)
+
+        def tab(lst, h):
+            o = 2048 + 512 * h
+            cp(T[lst][:, h * 64:(h + 1) * 64], T.ps[:, o:o + 64], [R("ps", o, o + 64)], [R(lst, h * 64, (h + 1) * 64)])
+
+        def give(lst):
+            send(B, "r" + lst, T[lst][:], T[lst][:], [R(lst)])
+
+        for t in range(7):
+            w, old = ("na", "nb")[t % 2], ("nb", "na")[t % 2]
+            src, ww, lst = ("invz", Z, "la") if t == 0 else (old, WZ, "nl%d" % (t - 1))
+            for h in range(2):
+                if h == 1 and t > 0:
+                    tab(lst, 1)
+                    give(lst)
+                for e, c in (("v", h * H), ("s", h * H + 512)):
+                    pick(e, w, c, src, 0, ww, lst, c // 16, 512)
+                rows(w, h)
+            tab("nl%d" % t, 0)
+        tab("nl6", 1)
+        give("nl6")
+        for h in range(2):
+            rows("invz", h)
+            tab("li", h)
+        give("li")
+        for c0, c1 in CH:
+            ts(T.fi[:, c0:c1], T.v7[:, c0:c1], 255, None, OP.bitwise_and, None, [R("v7", c0, c1)], [R("fi", c0, c1)])
+        for c0, c1 in CH:
+            ts(T.yo[:, c0:c1], T.fi[:, 0:WZ].indirect(T.li[:, c0 // 16:c1 // 16]), -1.0, 255.0, OP.mult, OP.add,
+               [R("fi"), R("li", c0 // 16, c1 // 16)], [R("yo", c0, c1)])
+            store(c0, c1)
+    else:
+        if l in hasQ:
+            near_pieces(qsrc, "lnq", solvers, Z, all_es)
+        addup(*FP, True)
+        addup(*FQ, True)
+        addup(*NP, True, plus=False)
+        addup(*FP, False)
+        addup(near, qsrc, "lnq", hasQ, 6, True, 1)
+        addup(*FQ, False)
+        far_p()
+        far_q()
+        fill("v7", -1)
+        fill("wa", 0.0)
+        fill("wb", 0.0)
+        addup(*NP, False, plus=False)
+        addup(near, qsrc, "lnq", hasQ, 6, False, 1)
+        addup(near, qsrc, "lnq", hasQ, 2, True, 0)
+        addup(near, qsrc, "lnq", hasQ, 2, False, 0)
+
+        def settle(dst, h, add, a, bank, o):
+            for b in range(2):
+                p, c0, d = (bank + b) * 512, h * H + 512 * b, a + 512 * b
+                tt(T[dst][:, c0:c0 + 512], T.ps[:, p:p + 512], T[add][:, d:d + 512], o,
+                   [R("ps", p, p + 512), R(add, d, d + 512)], [R(dst, c0, c0 + 512)])
+
+        def comb(dst, win, ww, lst, add, c0, c1, o):
+            tt(T[dst][:, c0:c1], T[win][:, 0:ww].indirect(T[lst][:, c0 // 16:c1 // 16]), T[add][:, c0:c1], o,
+               [R(win, 0, ww), R(lst), R(add, c0, c1)], [R(dst, c0, c1)])
+
+        settle("p1", 1, "rfp", H, 4, OP.subtract)
+        settle("q1", 1, "rfq", H, 6, OP.add)
+        for c0, c1 in ((0, 512), (512, H)):
+            tt(T.p1[:, c0:c1], T.rnp[:, c0:c1], T.rfp[:, c0:c1], OP.subtract, [R("rnp", c0, c1), R("rfp", c0, c1)], [R("p1", c0, c1)])
+        for t in range(7):
+            w, old = ("wa", "wb")[t % 2], ("wb", "wa")[t % 2]
+            for c0, c1 in ((H, Z), (0, H)):
+                if t == 0:
+                    if c0 == 0:
+                        settle("q1", 0, "rfq", 0, 2, OP.add)
+                    comb(w, "p1", Z, "lb", "q1", c0, c1, OP.add)
+                else:
+                    comb(w, old, WZ, "nl%d" % (t - 1), "vc", c0, c1, OP.add)
+                op("s", lambda: S.activation(T.vc[:, c0:c1], T[w][:, c0:c1], IDENT, bias=-1.0 if t == 6 else 0.0), [R(w, c0, c1)], [R("vc", c0, c1)])
+        for c, (c0, c1) in enumerate(CH):
+            comb("v7", "wa", WZ, "nl6", "vc", c0, c1, OP.add)
+            send(C[rank - 1], "rv%d" % c, T.v7[:, c0:c1], T.v7[:, c0:c1], [R("v7", c0, c1)])
+        hs = ((0, H), (H, Z))
+        for c0, c1 in hs:
+            comb("fi", "v7", WZ, "li", "p1", c0, c1, OP.subtract)
+        for c0, c1 in hs:
+            ts(T.fj[:, c0:c1], T.fi[:, c0:c1], 255, None, OP.bitwise_and, None, [R("fi", c0, c1)], [R("fj", c0, c1)])
+            cp(T.yo[:, c0:c1], T.fj[:, c0:c1], [R("fj", c0, c1)], [R("yo", c0, c1)])
+            store(c0, c1)
+    finish(sent[0])

@@ -6,28 +6,39 @@ COPY = ActivationFunctionType.Copy
 IDENT = ActivationFunctionType.Identity
 Z = 2048
 H = 1024
-WZ = Z + 256
-NL = 90
-LISTS = ["lb", "li"] + ["nl%d" % t for t in range(7)]
-CH = ((1024, 2048), (0, 512), (512, 1024))
+WZ = Z + 16
+NL = 87
+LISTS = ["li", "lm"] + ["nl%d" % t for t in range(6)]
+EARLY = ("nl0", "nl1")
+FAR = (("p", 0, 512, 0), ("p", 512, H, None), ("p", H, 1536, None), ("p", 1536, Z, None),
+       ("q", 0, 512, 0), ("q", 512, H, 0), ("q", H, 1536, None), ("q", 1536, Z, 0))
+TAIL = ((0, 256), (256, 768), (768, 1280), (1280, 1792), (1792, 2048))
+WFLOAT, IFLOAT = (0, 1, 2, 4), (0, 1, 2, 3, 4)
+LIFT = 2.0 ** 19
+CFG = {"ungated": (2, 2), "gate": 0, "arr": {"lfp": "JWM", "lfq": "MJW", "lnp": "WMJ", "lnq": "WMJ"}, "fpn": 0, "fqn": 2, "nq_own": 3, "relay_on": "", "i1": "sssss", "i2": "ssvsv", "lane": {}, "xn": 2, "fold": 0, "atw": {"W": "s", "I": "s", "J": "v"}, "fq_own": 4, "sa_at": 0, "lb_first": False, "wweave": (8, 0, 0, 0), "zm_early": 0, "sb_at": -1, "ddv": 0, "nq_before": 1, "weave": (0, 0, 0, 0), "merge": ("zm", "inw", "inv"), "xnear_first": True, "nq": 2, "wearly": True, "lnq_first": True, "split": 3, "s0": 2, "iq_first": 0,
+       }
+PAIR = (0, 2, 1, 3)
+CFG.update(x_es=("all", "all"), p_early=1, dd_early=0, wf=False, pev="svsv", ppk="svsv", i0="vvvvv", lag=(0, 0.1, 0.2, 1.05), self=(), iorder=(0, 1, 2, 3, 4), qi=False, xq=0, np_before=0, dm_early=(0, 0), marks=0, qorder=(0, 1, 2, 3), fold=0, i2="sssss", pi2=0, wweave=(3, 0, 0, 0), lb_first=False, nq=1, split=3, nq_own=2, relay_on="q")
 
 SCRATCH = {"ps": ("psum", [128, 4096], "float32")}
 for _names, _cols, _dt in (
-        ("xs qs", 4 * Z, "bfloat16"), ("lfp lfq lnp", 4 * H, "bfloat16"), ("lnq", 4 * Z, "bfloat16"),
-        ("zm yo dd iot inv invz", Z, "bfloat16"),
-        ("dm dp", 512, "bfloat16"), ("zeb bm bz base idb idn", 128, "bfloat16"), ("na nb", WZ, "bfloat16"), ("il", 256, "bfloat16"),
+        ("xs qs lfp lfq lnp lnq", 4 * Z, "bfloat16"),
+        ("zm yo dd inv inw invz", Z, "bfloat16"), ("iot", Z, "bfloat16"),
+        ("dm", 512, "bfloat16"), ("zeb bm bz base idb", 128, "bfloat16"), ("na nb", WZ, "bfloat16"), ("il", 256, "bfloat16"),
         ("pin", 512, "int32"), ("losti", 2, "int32"), ("zin i1 i3", 128, "int32"), ("i2 i2b", 16, "int32"),
-        ("i4 i4b i4c", 4, "int32"), ("i5", 8, "int32"), ("v7 fi", WZ, "int32"), ("fj", Z, "int32"),
-        ("lp", 512, "uint16"), (" ".join(LISTS) + " la", 128, "uint16"),
-        ("ph", 512, "float16"), ("lpi sa sb", 768, "float16"), ("idh", 128, "float16"),
-        ("rfp rfq", Z, "float16"), ("fsp fsq relay", H, "float16"), ("nsp rnp", H, "float32"),
-        ("lostf", 2, "float32"), ("kcol odd even wcol", 4, "float32"), ("rmask", 16, "float32"), ("ea eb ms mn mp bev", 8, "float32"),
-        ("p1 q1 vc", Z, "float32"), ("wa wb", WZ, "float32")):
+        ("i4 i4b i4c", 4, "int32"), ("i5", 8, "int32"), ("fi fj", Z, "int32"),
+        ("lp lq", 512, "uint16"), (" ".join(LISTS) + "", 128, "uint16"), ("lb", 384, "uint16"),
+        ("ph", 512, "float16"), ("sa sb", 768, "float16"), ("lpi", 1536, "float16"), ("idh", 128, "float16"),
+        ("rfp rfq fsp fsq", Z, "float16"),
+        ("lostf", 2, "float32"), ("idf", 128, "float32"), ("kcol odd even wcol", 4, "float32"), ("rmask", 16, "float32"), ("ea eb ms mn bev", 8, "float32"),
+        ("p1 pb vc raw qq", Z, "float32"), ("wa wb", WZ, "float32")):
     for _n in _names.split():
         SCRATCH[_n] = ("sbuf", [128, _cols], _dt)
-SEMAPHORES = (["l%d" % i for i in range(NL)] + ["snt", "rpi", "rrelay"]
-              + ["r%s%d" % (b, s) for b in ("lfp", "lfq", "lnp", "lnq") for s in range(4)]
-              + ["rrfp0", "rrfp1", "rrfq0", "rrfq1", "rrnp", "rv0", "rv1", "rv2"] + ["r" + n for n in LISTS])
+SEMAPHORES = (["l%d" % i for i in range(NL)] + ["snt", "rpi", "rinw", "rp1", "rwa0", "rwa1", "rlf"]
+              + ["r%s%d" % (b, s) for b in ("lnp", "lnq") for s in range(4)]
+              + ["r%s%d%d" % (b, s, h) for b in ("lfp", "lfq") for s in range(4) for h in range(2)]
+              + ["rfar%d" % i for i in range(len(FAR))] + ["rrelay%d" % i for i in range(len(FAR))]
+              + ["rz%d" % i for i in range(len(TAIL))] + ["r" + n for n in LISTS] + ["rh" + n for n in EARLY])
 
 
 def tracker(g, T):
@@ -119,27 +130,45 @@ def bits(es):
     return sum(1 << e for e in es)
 
 
-def relay_of(core, T, topo):
+def relay_of(core, j, T, topo):
     cs = topo.cores_of(core)
     same = [c for c in cs if T.rank_of(c) is not None and topo.die(c) == topo.die(core)]
     free = [c for c in cs if T.rank_of(c) is None and topo.die(c) != topo.die(core)]
-    return free[same.index(core)]
+    return free[same.index(core) + j]
+
+
+def far_solver(core, C, topo):
+    here = [c for c in C if topo.chip(c) == topo.chip(core)]
+    zs = [z for z in range(4) if C[2 * z] not in here]
+    return C[2 * zs[here.index(core) // 2]]
+
+
+def relay_engines(c, to, relay, topo):
+    return [e for e in topo.engines(c, relay) if e not in topo.engines(c, to)]
+
+
+def hop_lanes(kind, all_es, off_es):
+    if CFG["relay_on"] == "all":
+        return all_es
+    return [e for e in all_es if e not in off_es] if kind in CFG["relay_on"] else off_es
 
 
 def rank_program(g, core, T, topo):
     rank = T.rank_of(core)
     C = list(T.cores)
     if rank is None:
+        n = 0
         for c in C[0::2]:
-            if topo.chip(c) == topo.chip(core) and relay_of(c, T, topo) == core:
-                here = [d for d in C if topo.chip(d) == topo.chip(c)]
-                zs = [z for z in range(4) if C[2 * z] not in here]
-                to = C[2 * zs[here.index(c) // 2] + 1]
-                a = topo.addr(to)
-                g.wait_ge(T.sem["rrelay"], len(topo.engines(c, to)))
-                g.remote_dma(out_ap=T.rfp[:, 0:H], in_ap=T.relay[:], remote_sem=T.sem["rrfp0"],
-                             local_sem=T.sem["snt"], pid=a[1], routing_id=a[0], dma_engine_mask=topo.mask(core, to))
-                g.wait_ge(T.sem["snt"], len(topo.engines(core, to)))
+            for i, (kind, c0, c1, via) in enumerate(FAR):
+                if topo.chip(c) == topo.chip(core) and via is not None and relay_of(c, via, T, topo) == core:
+                    to = far_solver(c, C, topo)
+                    a = topo.addr(C[C.index(to) + 1] if CFG["wf"] and kind == "p" else to)
+                    g.wait_ge(T.sem["rrelay%d" % i], len(hop_lanes(kind, topo.engines(c, core), topo.engines(c, to))))
+                    g.remote_dma(out_ap=T["rf" + kind][:, c0:c1], in_ap=T["fs" + kind][:, c0:c1], remote_sem=T.sem["rfar%d" % i],
+                                 local_sem=T.sem["snt"], pid=a[1], routing_id=a[0], dma_engine_mask=topo.mask(core, to))
+                    n += len(topo.engines(core, to))
+        if n:
+            g.wait_ge(T.sem["snt"], n)
         return
     V, S, PE = g.vector, g.scalar, g.tensor
     op, batch, landing, reading, finish = tracker(g, T)
@@ -147,16 +176,19 @@ def rank_program(g, core, T, topo):
     l = local.index(rank)
     near = sorted({r // 2 for r in local})
     far = [z for z in range(4) if z not in near]
-    isA = rank % 2 == 0
+    isW = rank % 2 == 0
     zone = rank // 2
     data = rank < 6
     hasP = [s for s in range(4) if local[s] != 7]
     hasQ = [s for s in range(4) if local[s] != 6]
-    others = [d for d in range(4) if d != l]
     away = [r for r in range(8) if r not in local]
-    all_es = topo.engines(core, C[local[others[0]]])
+    all_es = topo.engines(core, C[local[l ^ 1]])
     off_es = topo.engines(core, C[away[0]])
     on_es = [e for e in all_es if e not in off_es]
+    SPLIT = CFG["split"]
+    mine = list(range(8 - SPLIT, 8) if isW else range(8 - SPLIT))
+    NQ = CFG["nq"]
+    QW = Z // NQ
     sent = [0]
 
     def R(b, a=0, z=None):
@@ -173,30 +205,65 @@ def rank_program(g, core, T, topo):
     def send_all(parts, reads):
         reading("g", reads)
         trs = []
-        for r, sem, dst, src, es in parts:
-            a = topo.addr(C[r])
-            trs.append(RemoteDMATransfer(dst_ids=[DstId(rid=a[0], pnc=a[1])], dma_engine_mask=bits(es),
-                                         remote_sem=T.sem[sem], src=src, dst=dst))
+        for rs, sem, dst, srcs, es in parts:
+            ids = [DstId(rid=topo.addr(C[r])[0], pnc=topo.addr(C[r])[1]) for r in rs]
+            trs.append(RemoteDMATransfer(dst_ids=ids, dma_engine_mask=bits(es), remote_sem=T.sem[sem],
+                                         srcs=srcs, dsts=[dst] * len(rs), alu_op=1 if len(srcs) > 1 else 0))
             sent[0] += len(es)
         g.remote_dma_fused(trs, local_sem=T.sem["snt"])
 
-    def width(r):
-        return len(topo.engines(C[r], core))
-    for b, who, w, n in (("lfp", hasP, H, 4), ("lfq", hasQ, H, 4), ("lnp", hasP, H, len(on_es)), ("lnq", hasQ, Z, len(all_es))):
-        for s in who:
-            if s != l and not (isA and b == "lnq"):
-                landing(b, s * w, (s + 1) * w, "r%s%d" % (b, s), n)
-    if isA:
-        landing("lpi", 0, 768, "rpi", 4 * (5 if data else 6))
-        for c, (c0, c1) in enumerate(CH):
-            landing("v7", c0, c1, "rv%d" % c, width(rank + 1))
-    else:
+    def at_w(s, w):
+        return local[s] < 6 and s != w and CFG["atw"].get("W" if s % 2 == 0 else "I" if s == w + 1 else "J")
+
+    full = len(all_es)
+    WF = CFG["wf"]
+    LW = 384 if WF else 256
+    x_es = [{"on": on_es, "off": off_es, "all": all_es}[k] for k in CFG["x_es"]]
+
+    def list_es(n):
+        return on_es if WF else all_es
+    QI = CFG["qi"] or WF
+    for i, (kind, c0, c1, via) in enumerate(FAR):
+        if isW != (WF and kind == "p"):
+            landing("rf" + kind, c0, c1, "rfar%d" % i, len(off_es))
+    q_es = off_es if CFG["xq"] else all_es
+    if isW != QI:
+        for s in hasQ:
+            if s != l:
+                for h in range(NQ):
+                    landing("lfq", s * Z + h * QW, s * Z + (h + 1) * QW, "rlfq%d%d" % (s, h), len(q_es) // 2 if s % 2 != l % 2 else len(q_es))
+    def lanes(b, s, w):
+        kind = CFG["lane"].get(b + ("W" if s % 2 == 0 else "I" if s == w + 1 else "J"), "on")
+        return {"on": on_es, "off": off_es, "all": all_es}[kind]
+    if isW:
+        landing("lpi", 0, 1536, "rpi", 4 * (5 if data else 6))
+        for s in range(4):
+            if s != l:
+                for b, who in (("lnp", hasP), ("lnq", hasQ)):
+                    if s in who and not (b == "lnq" and at_w(s, l)):
+                        landing(b, s * Z, (s + 1) * Z, "r%s%d" % (b, s), len(lanes(b, s, l)))
         for n in LISTS:
-            landing(n, 0, 128, "r" + n, width(rank - 1))
-        landing("rnp", 0, H, "rrnp", width(rank - 1))
-        for b in ("rfp", "rfq"):
+            if n in EARLY:
+                landing(n, 0, 64, "rh" + n, len(list_es(n)))
+                landing(n, 64, 128, "r" + n, len(list_es(n)))
+            else:
+                landing(n, 0, 128, "r" + n, len(list_es(n)))
+    else:
+        for s in hasP:
+            if s != l:
+                for h in range(2):
+                    landing("lfp", s * Z + h * H, s * Z + (h + 1) * H, "rlfp%d%d" % (s, h), len(x_es[h]) // (1 if s % 2 else 2))
+        landing("lb", 0, 384, "rpi", len(off_es))
+        if not CFG["fold"]:
+            landing("p1", 0, Z, "rp1", full)
+        if SPLIT:
+            landing("inw", 0, Z, "rinw", full)
+        for i, (c0, c1) in enumerate(TAIL):
+            if i not in CFG["self"]:
+                landing("raw", c0, c1, "rz%d" % i, full)
+        if CFG["self"]:
             for h in range(2):
-                landing(b, h * H, (h + 1) * H, "r%s%d" % (b, h), width(away[0]))
+                landing("wa", h * H, (h + 1) * H, "rwa%d" % h, full)
 
     def load(e, dst, src, w):
         q = g.sync if e == "y" else S
@@ -204,26 +271,28 @@ def rank_program(g, core, T, topo):
 
     def loadx(e, z):
         load(e, T.xs[:, z * Z:(z + 1) * Z], T.x[:, z * Z:(z + 1) * Z], R("xs", z * Z, (z + 1) * Z))
-    mine_first = sorted(near, key=lambda z: z != zone)
+    fars = sorted(far, key=lambda z: z == far[l // 2])
+    nears = sorted(near, key=lambda z: (z == zone) == isW)
     if data:
         load("y", T.pin[:], T.pi[:], R("pin"))
     load("s", T.losti[:], T.lost[:], R("losti"))
-    if isA:
+    if not isW:
         load("s", T.zin[:], T.zero[:], R("zin"))
-    loadx("y", far[0])
-    loadx("s", far[1])
-    for z in mine_first:
+    loadx("y", fars[0])
+    loadx("s", fars[1])
+    ungated = CFG["ungated"][0 if isW else 1] if data else 2
+    for z in nears[:ungated]:
         loadx("y", z)
 
     def iota(b, pattern, base, cm, **kw):
         op("g", lambda: g.iota(T[b][:], pattern, base, cm, **kw), [], [R(b)])
     iota("i1", [[-1, 128]], 0, 1)
     iota("i5", [[1, 8]], 0, 0)
-    if isA:
+    iota("i4", [[0, 4]], 0, 1)
+    iota("il", [[1, 256]], 0, 0, allow_small_or_imprecise_dtypes=True)
+    if not isW:
         iota("i2", [[-1, 16]], 16, 1)
         iota("i3", [[1, 8], [0, 16]], 0, 0)
-        iota("i4", [[0, 4]], 0, 1)
-        iota("il", [[1, 256]], 0, 0, allow_small_or_imprecise_dtypes=True)
 
     def ts(out, in0, s1, s2, op0, op1, reads, writes):
         a = (out, in0, s1, s2, op0) if op1 is None else (out, in0, s1, s2, op0, op1)
@@ -232,8 +301,11 @@ def rank_program(g, core, T, topo):
     def tt(out, in0, in1, o, reads, writes):
         op("v", lambda: V.tensor_tensor(out, in0, in1, o), reads, writes)
 
-    def cp(out, in_, reads, writes):
-        op("v", lambda: V.tensor_copy(out, in_), reads, writes)
+    def cp(out, in_, reads, writes, e="v"):
+        if e == "v":
+            op("v", lambda: V.tensor_copy(out, in_), reads, writes)
+        else:
+            op("s", lambda: S.activation(out, in_, COPY), reads, writes)
 
     def fill(b, c, a=Z, z=WZ):
         op("v", lambda: V.memset(T[b][:, a:z], c), [], [(b, a, z)])
@@ -246,263 +318,482 @@ def rank_program(g, core, T, topo):
                           [R(idn), R(b)], [R(dst, i * 128, (i + 1) * 128)]))
         batch("v", items)
 
-    if isA:
-        fill("dd", 0.0, 0, Z)
-    ts(T.idb[:], T.i1[:], 0, None, OP.is_equal, None, [R("i1")], [R("idb")])
-    if isA:
+    def spread_zero(p0, p1):
+        batch("s", [(lambda p=p: S.activation(T.zm[:, p:Z:16], T.zeb[:], COPY, scale=T.rmask[:, p:p + 1]),
+                     [R("zeb"), R("rmask")], [R("zm")]) for p in range(p0, p1)])
+
+    if 0 < SPLIT < 8:
+        fill("inv", 0.0, 0, Z)
+    ts(T.i4c[:], T.i4[:], 1, None, OP.bitwise_and, None, [R("i4")], [R("i4c")])
+    if isW:
         ts(T.idh[:], T.i1[:], 0, None, OP.is_equal, None, [R("i1")], [R("idh")])
+    cp(T.odd[:], T.i4c[:], [R("i4c")], [R("odd")])
+    ts(T.even[:], T.i4c[:], 0, None, OP.is_equal, None, [R("i4c")], [R("even")])
+    ts(T.idb[:], T.i1[:], 0, None, OP.is_equal, None, [R("i1")], [R("idb")])
+    ts(T.bev[:], T.i5[:], T.even[:, 0:1], None, OP.mult, None, [R("i5"), R("even")], [R("bev")])
+    if mine:
+        batch("s", [(lambda b=b: S.activation(T.iot[:, b * 256:(b + 1) * 256], T.il[:], IDENT, scale=T.odd[:, 0:1], bias=T.bev[:, b:b + 1]),
+                     [R("il"), R("odd"), R("bev")], [R("iot", b * 256, (b + 1) * 256)]) for b in mine])
+    if isW:
+        fill("wa", 0.0)
+        fill("wb", 0.0)
+    else:
         ts(T.i2b[:], T.i2[:], 15, None, OP.bitwise_and, None, [R("i2")], [R("i2b")])
         ts(T.i4b[:], T.i4[:], 4, None, OP.arith_shift_right, None, [R("i4")], [R("i4b")])
-        ts(T.i4c[:], T.i4[:], 1, None, OP.bitwise_and, None, [R("i4")], [R("i4c")])
         ts(T.rmask[:], T.i2b[:], 0, None, OP.is_equal, None, [R("i2b")], [R("rmask")])
         cp(T.kcol[:], T.i4b[:], [R("i4b")], [R("kcol")])
-        cp(T.odd[:], T.i4c[:], [R("i4c")], [R("odd")])
+
+    def marks():
+        cp(T.lostf[:], T.losti[:], [R("losti")], [R("lostf")])
+        ts(T.eb[:], T.i5[:], T.lostf[:, 1:2], None, OP.is_equal, None, [R("i5"), R("lostf")], [R("eb")])
+        ts(T.ea[:], T.i5[:], T.lostf[:, 0:1], None, OP.is_equal, None, [R("i5"), R("lostf")], [R("ea")])
+    if CFG["marks"]:
+        marks()
     if data:
-        cp(T.ph[:], T.pin[:], [R("pin")], [R("ph")])
-        where = [(2 * z, off_es[4 * i:4 * i + 4]) for i, z in enumerate(far)]
-        where += [(r, on_es[4 * i:4 * i + 4]) for i, r in enumerate(2 * z for z in near if 2 * z != rank)]
-        send_all([(r, "rpi", T.lpi[:, rank * 128:(rank + 1) * 128], T.ph[:, (r // 2) * 128:(r // 2 + 1) * 128], es)
-                  for r, es in where], [R("ph")])
+        for z0, z1 in ((0, 1), (1, 2), (2, 3), (3, 4)) if WF else ():
+            cp(T.ph[:, PAIR[z0] * 128:PAIR[z0] * 128 + 128], T.pin[:, z0 * 128:z1 * 128], [R("pin")], [R("ph", PAIR[z0] * 128, PAIR[z0] * 128 + 128)])
+        if not WF:
+            cp(T.ph[:], T.pin[:], [R("pin")], [R("ph")])
+        where = [(z, off_es[4 * i:4 * i + 4]) for i, z in enumerate(far)] + [(z, on_es[4 * i:4 * i + 4]) for i, z in enumerate(near)]
+        for part in ((where[:2], where[2:]) if CFG["pi2"] else (where,)):
+            send_all([([2 * z], "rpi", T.lpi[:, rank * 256:(rank + 1) * 256] if WF else T.lpi[:, rank * 256 + z // 2 * 128:rank * 256 + z // 2 * 128 + 128],
+                       [T.ph[:, z % 2 * 256:z % 2 * 256 + 256] if WF else T.ph[:, z * 128:z * 128 + 128]], es) for z, es in part if 2 * z != rank], [R("ph")])
+    if data:
         cp(T.lp[:], T.pin[:], [R("pin")], [R("lp")])
-    cp(T.lostf[:], T.losti[:], [R("losti")], [R("lostf")])
-    ts(T.ea[:], T.i5[:], T.lostf[:, 0:1], None, OP.is_equal, None, [R("i5"), R("lostf")], [R("ea")])
-    ts(T.eb[:], T.i5[:], T.lostf[:, 1:2], None, OP.is_equal, None, [R("i5"), R("lostf")], [R("eb")])
+    if not CFG["marks"]:
+        marks()
     tt(T.ms[:], T.ea[:], T.eb[:], OP.add, [R("ea"), R("eb")], [R("ms")])
     ts(T.mn[:], T.ms[:], -1.0, None, OP.add, None, [R("ms")], [R("mn")])
-    nd = len([r for r in local if r < 6])
-    scaled(nd, "dm", "idb", lambda i: ("mn", local[i]))
 
-    def weight(s, plus):
-        m, i = ("dm", "idb") if plus else ("dp", "idn")
-        return (T[m][:, s * 128:(s + 1) * 128], R(m, s * 128, (s + 1) * 128)) if local[s] < 6 else (T[i][:], R(i))
+    def masks():
+        batch("s", [(lambda i=i, r=r: S.activation(T.dm[:, i * 128:(i + 1) * 128], T.idb[:], COPY, scale=T.mn[:, r:r + 1]),
+                     [R("idb"), R("mn")], [R("dm", i * 128, (i + 1) * 128)]) for i, r in enumerate(local) if r < 6])
+    if CFG["dm_early"][0 if isW else 1]:
+        masks()
+    if not isW and CFG["zm_early"]:
+        cp(T.zeb[:], T.zin[:], [R("zin")], [R("zeb")])
+        spread_zero(0, CFG["zm_early"])
 
-    def pick(e, dst, d0, src, s0, s1, lst, t0, n):
+    def weights(h):
+        if isW and CFG["sb_at"] == h:
+            scaled(6, "sb", "idh", lambda i: ("eb", i))
+        if isW and CFG["sa_at"] == h:
+            scaled(6, "sa", "idh", lambda i: ("ea", i))
+    weights(-1)
+
+    def pick(e, dst, d0, src, s0, s1, lst, t0, n, bias=None):
         out, in_ = T[dst][:, d0:d0 + n], T[src][:, s0:s1].indirect(T[lst][:, t0:t0 + n // 16])
         rd, wr = [R(src, s0, s1), R(lst, t0, t0 + n // 16)], [R(dst, d0, d0 + n)]
         if e == "v":
             op("v", lambda: V.tensor_copy(out, in_), rd, wr)
-        else:
+        elif bias is None:
             op("s", lambda: S.activation(out, in_, COPY), rd, wr)
+        else:
+            op("s", lambda: S.activation(out, in_, IDENT, bias=bias), rd, wr)
 
-    def gather(e, z):
-        pick(e, "qs", z * Z, "xs", z * Z, (z + 1) * Z, "lp", z * 128, Z)
+    def gather(e, z, c0=0, c1=Z):
+        if data:
+            pick(e, "qs", z * Z + c0, "xs", z * Z, (z + 1) * Z, "lp", z * 128 + c0 // 16, c1 - c0)
 
-    def piece(zs, srcb, landb, d, w, es):
-        a = zs[d // 2] * Z + (d % 2 * H if w == H else 0)
-        return (local[d], "r%s%d" % (landb, l), T[landb][:, l * w:(l + 1) * w], T[srcb][:, a:a + w], es), R(srcb, a, a + w)
+    def adder(z, landb="lfq"):
+        return local[2 * near.index(z) if z in near else 2 * far.index(z) + (landb == "lfp" or QI)]
 
-    def far_pieces(srcb, landb):
-        ps = [piece(far, srcb, landb, d, H, topo.engines(core, C[local[d]])[4 * i:4 * i + 4]) for i, d in enumerate(others)]
-        send_all([p[0] for p in ps], [p[1] for p in ps])
-
-    def near_pieces(srcb, landb, to, w, es):
-        for d in sorted(to, key=lambda d: d // 2 != l // 2):
-            (r, sem, dst, src, es), rd = piece(near, srcb, landb, d, w, es)
-            send(C[r], sem, dst, src, [rd], es)
+    def hand(z, srcb, landb):
+        if adder(z, landb) != rank:
+            send(C[adder(z, landb)], "r%s%d" % (landb, l), T[landb][:, l * Z:(l + 1) * Z], T[srcb][:, z * Z:(z + 1) * Z],
+                 [R(srcb, z * Z, (z + 1) * Z)], lanes(landb, l, local.index(adder(z))))
 
     qsrc = "qs" if data else "xs"
-    if data:
-        gather("v", far[0])
-        gather("s", far[1])
+
+    def far_q(h):
+        zs = [z for z in fars if adder(z) != rank]
+        n = len(q_es) // len(zs)
+        send_all([([adder(z)], "rlfq%d%d" % (l, h), T.lfq[:, l * Z + h * QW:l * Z + (h + 1) * QW],
+                   [T[qsrc][:, z * Z + h * QW:z * Z + (h + 1) * QW]], q_es[i * n:(i + 1) * n]) for i, z in enumerate(zs)],
+                 [R(qsrc, z * Z + h * QW, z * Z + (h + 1) * QW) for z in zs])
+
+    for h in range(NQ):
+        gather("v", fars[0], h * QW, (h + 1) * QW)
+        gather("s", fars[1], h * QW, (h + 1) * QW)
+        weights(h)
+    if not CFG["dm_early"][0 if isW else 1]:
+        masks()
+    for z in nears[ungated:]:
+        a = fars[0] * Z + CFG["gate"]
+        op("y", lambda: g.sync.dma_start(T.xs[:, z * Z:(z + 1) * Z], T.x[:, z * Z:(z + 1) * Z]), [R("qs", a, a + 16)], [R("xs", z * Z, (z + 1) * Z)], True)
     if l in hasP:
-        far_pieces("xs", "lfp")
+        zs = [z for z in fars if adder(z, "lfp") != rank]
+        for h in range(2):
+            n = len(x_es[h]) // len(zs)
+            send_all([([adder(z, "lfp")], "rlfp%d%d" % (l, h), T.lfp[:, l * Z + h * H:l * Z + (h + 1) * H],
+                       [T.xs[:, z * Z + h * H:z * Z + (h + 1) * H]], x_es[h][i * n:(i + 1) * n]) for i, z in enumerate(zs)],
+                     [R("xs", z * Z + h * H, z * Z + (h + 1) * H) for z in zs])
+    handed = []
+
+    def near_x(zs=nears):
+        if l in hasP:
+            for z in zs:
+                if z not in handed:
+                    hand(z, "xs", "lnp")
+                    handed.append(z)
+    near_x(nears[:CFG["xq"]])
     if l in hasQ:
-        far_pieces(qsrc, "lfq")
-    if l in hasP:
-        near_pieces("xs", "lnp", others, H, on_es)
-    if not isA:
-        ts(T.mp[:], T.mn[:], -1.0, None, OP.mult, None, [R("mn")], [R("mp")])
-        scaled(nd, "dp", "idb", lambda i: ("mp", local[i]))
-        ts(T.idn[:], T.idb[:], -1.0, None, OP.mult, None, [R("idb")], [R("idn")])
-    if data:
-        gather("s", mine_first[0])
-        gather("s" if isA else "v", mine_first[1])
-
-    def addup(zs, srcb, landb, who, bank, mine, half=None, plus=True):
-        items = []
-        z, w, d, h = (zs[l // 2], H, 0, l % 2) if half is None else (zone, Z, half * H, half)
-        seq = [s for s in who if s == l] + [s for s in who if s != l]
-        for n, s in enumerate(seq):
-            if (s == l) != mine:
-                continue
-            wt, wr = weight(s, plus)
-            for b in range(2):
-                buf, a = (srcb, z * Z + h * H + 512 * b) if s == l else (landb, s * w + d + 512 * b)
-                o = (bank + b) * 512
-                items.append((lambda o=o, wt=wt, buf=buf, a=a, st=n == 0, en=n == len(seq) - 1:
-                              PE.matmul(T.ps[:, o:o + 512], wt, T[buf][:, a:a + 512], st, en),
-                              [wr, R(buf, a, a + 512)], [R("ps", o, o + 512)]))
-        if items:
-            batch("t", items, acc=True)
-
-    def evac(dst, bank):
-        for b in range(2):
-            o = (bank + b) * 512
-            ts(T[dst][:, b * 512:b * 512 + 512], T.ps[:, o:o + 512], 1.0, None, OP.add, None, [R("ps", o, o + 512)], [R(dst, b * 512, b * 512 + 512)])
-
-    def far_send(src, dst):
-        h = l % 2
-        send(C[2 * far[l // 2] + 1], "r%s%d" % (dst, h), T[dst][:, h * H:(h + 1) * H], T[src][:], [R(src)])
-
-    def far_p():
-        evac("fsp", 0)
-        if isA:
-            send(relay_of(core, T, topo), "rrelay", T.relay[:], T.fsp[:], [R("fsp")], off_es)
-        else:
-            far_send("fsp", "rfp")
-
-    def far_q():
-        evac("fsq", 2)
-        far_send("fsq", "rfq")
+        for h in range(NQ):
+            far_q(h)
 
     def store(c0, c1):
         op("y", lambda: g.sync.dma_start(T.y[:, c0:c1], T.yo[:, c0:c1]), [R("yo", c0, c1)], [], True)
 
-    FP, FQ = (far, "xs", "lfp", hasP, 0), (far, qsrc, "lfq", hasQ, 2)
-    NP = (near, "xs", "lnp", hasP, 4)
-    solvers = [d for d in others if d % 2 == 1]
-    if isA:
-        B = C[rank + 1]
-        cp(T.zeb[:], T.zin[:], [R("zin")], [R("zeb")])
-        scaled(6, "sb", "idh", lambda i: ("eb", i))
-        scaled(6, "sa", "idh", lambda i: ("ea", i))
-        ts(T.even[:], T.i4c[:], 0, None, OP.is_equal, None, [R("i4c")], [R("even")])
+    def comb(dst, win, lst, add, c0, c1):
+        tt(T[dst][:, c0:c1], T[win][:, 0:WZ].indirect(T[lst][:, c0 // 16:c1 // 16]), T[add][:, c0:c1], OP.add,
+           [R(win, 0, WZ), R(lst, c0 // 16, c1 // 16), R(add, c0, c1)], [R(dst, c0, c1)])
+
+    def last_step(i, e):
+        c0, c1 = TAIL[i]
+        if e == "s":
+            pick("s", "vc", c0, "wa", 0, WZ, "li", c0 // 16, c1 - c0, LIFT)
+        else:
+            comb("raw", "wa", "lm", "vc", c0, c1)
+
+    def affine(e, out, in_, scale, bias, reads, writes):
+        if e == "v":
+            ts(out, in_, scale, bias, OP.mult, OP.add, reads, writes)
+        else:
+            op("s", lambda: S.activation(out, in_, IDENT, scale=scale, bias=bias), reads, writes)
+
+    def round_down(i, sign, e1="s", e2="s"):
+        c0, c1 = TAIL[i]
+        o = 512 * i
+        affine(e1, T.qq[:, c0:c1], T.raw[:, c0:c1], (1 + sign * 2.0 ** -20) / 256, 2.0 ** 23 - 0.5, [R("raw", c0, c1)], [R("qq", c0, c1)])
+        affine(e2, T.ps[:, o:o + c1 - c0], T.qq[:, c0:c1], -256.0 * sign, 2.0 ** 31 if sign > 0 else 256 - 2.0 ** 31,
+               [R("qq", c0, c1)], [R("ps", o, o + 512)])
+
+    def rest(i, sign):
+        c0, c1 = TAIL[i]
+        o = 512 * i
+        tt(T.yo[:, c0:c1], T.ps[:, o:o + c1 - c0], T.raw[:, c0:c1], OP.add if sign > 0 else OP.subtract,
+           [R("ps", o, o + 512), R("raw", c0, c1)], [R("yo", c0, c1)])
+        store(c0, c1)
+
+    def by_bits(i, sign):
+        c0, c1 = TAIL[i]
+        ts(T.fi[:, c0:c1], T.raw[:, c0:c1], float(sign), None, OP.mult, None, [R("raw", c0, c1)], [R("fi", c0, c1)])
+        ts(T.fj[:, c0:c1], T.fi[:, c0:c1], 255, None, OP.bitwise_and, None, [R("fi", c0, c1)], [R("fj", c0, c1)])
+        cp(T.yo[:, c0:c1], T.fj[:, c0:c1], [R("fj", c0, c1)], [R("yo", c0, c1)])
+        store(c0, c1)
+
+    def choose():
+        items = []
+        for nm, o, z in (("sb", 3584, zone), ("sa", 3712, zone), ("sb", 3840, fz))[:2 + WF]:
+            for i in range(6):
+                buf, a = ("ph", (PAIR[z] if WF else z) * 128) if i == rank else ("lpi", i * 256 + z // 2 * 128)
+                items.append((lambda i=i, buf=buf, a=a, nm=nm, o=o: PE.matmul(T.ps[:, o:o + 128], T[nm][:, i * 128:(i + 1) * 128], T[buf][:, a:a + 128], i == 0, i == 5),
+                              [R(nm, i * 128, (i + 1) * 128), R(buf, a, a + 128)], [R("ps", o, o + 128)]))
+        batch("t", items, acc=True)
+        cp(T.lb[:, 0:LW], T.ps[:, 3584:3584 + LW], [R("ps", 3584, 3968)], [R("lb")])
+
+    def scat(bs):
+        if bs:
+            a, z = bs[0], bs[-1] + 1
+            cp(T.inv[:, 0:Z].indirect(T.lb[:, a * 16:z * 16]), T.iot[:, a * 256:z * 256], [R("lb"), R("iot")], [R("inv")])
+
+    fz = far[l // 2]
+    to = far_solver(core, C, topo)
+    others = [s for s in range(4) if s != l]
+    picks = [z for z in nears if not at_w(l, local.index(adder(z)))]
+
+    def arrival(landb):
+        who = {"M": l ^ 1, "W": (l ^ 2) & 2, "J": (l ^ 2) | 1}
+        return [who[c] for c in CFG["arr"][landb]]
+
+    def add_landed(job, n, last=None):
+        for s in arrival(job[2])[:n]:
+            addup(*job, [s], last=last)
+        addup(*job, arrival(job[2])[n:], last=last)
+
+    def weight(s):
+        return (T.dm[:, s * 128:(s + 1) * 128], R("dm", s * 128, (s + 1) * 128)) if local[s] < 6 else (T.idb[:], R("idb"))
+
+    def addup(z, srcb, landb, who, bank, part, banks=range(4), last=None):
+        seq = [s for s in [l] + arrival(landb) if s in who] + ([last] if last else [])
+        for b in banks:
+            items = []
+            for n, s in enumerate(seq):
+                if s in part:
+                    wt, wr = (T.idh[:], R("idh")) if s == last else weight(s)
+                    buf, a = (last, 512 * b) if s == last else (srcb, z * Z + 512 * b) if s == l else (landb, s * Z + 512 * b)
+                    o = (bank + b) * 512
+                    items.append((lambda o=o, wt=wt, buf=buf, a=a, n=n: PE.matmul(T.ps[:, o:o + 512], wt, T[buf][:, a:a + 512], n == 0, n == len(seq) - 1),
+                                  [wr, R(buf, a, a + 512)], [R("ps", o, o + 512)]))
+            if items:
+                batch("t", items, acc=True)
+
+    def far_piece(i):
+        kind, c0, c1, via = FAR[i]
+        src, o = "fs" + kind, Z * (kind == "q")
+        for c in range(c0, c1, 512):
+            if WF and kind == "q":
+                tt(T[src][:, c:c + 512], T.ps[:, o + c:o + c + 512], T.vc[:, c:c + 512], OP.subtract,
+                   [R("ps", o + c, o + c + 512), R("vc", c, c + 512)], [R(src, c, c + 512)])
+            elif not WF:
+                cp(T[src][:, c:c + 512], T.ps[:, o + c:o + c + 512], [R("ps", o + c, o + c + 512)], [R(src, c, c + 512)])
+        if via is None:
+            send(C[C.index(to) + 1] if WF and kind == "p" else to, "rfar%d" % i, T["rf" + kind][:, c0:c1], T[src][:, c0:c1], [R(src, c0, c1)])
+        else:
+            rl = relay_of(C[2 * zone], via, T, topo)
+            send(rl, "rrelay%d" % i, T[src][:, c0:c1], T[src][:, c0:c1], [R(src, c0, c1)], hop_lanes(kind, all_es, off_es))
+
+    def far_pieces(which):
+        for i, f in enumerate(FAR):
+            if f[0] == which:
+                far_piece(i)
+
+    if not isW:
+        W = C[rank - 1]
+
+        def give(lst, h=None):
+            c0, c1 = (0, 128) if h is None else (64 * h, 64 * h + 64)
+            send(W, ("rh" if h == 0 else "r") + lst, T[lst][:, c0:c1], T[lst][:, c0:c1], [R(lst, c0, c1)], list_es(lst))
+
+        def far_p(b):
+            c = 512 * b
+            cp(T.fsp[:, c:c + 512], T.ps[:, c:c + 512], [R("ps", c, c + 512)], [R("fsp", c, c + 512)])
+            for i, f in enumerate(FAR):
+                if f[0] == "p" and c < f[2] <= c + 512:
+                    far_piece(i)
+
+        FP, FQ = (fz, "xs", "lfp", hasP, 0), (fz, qsrc, "lfq", hasQ, 4)
+        if not data and l in hasQ:
+            for z in nears:
+                hand(z, qsrc, "lnq")
+        addup(*FP, [l])
+        if QI:
+            addup(*FQ, [l])
+        if not CFG["zm_early"]:
+            cp(T.zeb[:], T.zin[:], [R("zin")], [R("zeb")])
+        fill("bz", 0.0, 0, 128)
+        for nm in ("na", "nb"):
+            fill(nm, 8.0)
         ts(T.bm[:], T.i3[:], T.kcol[:, 0:1], None, OP.is_equal, None, [R("i3"), R("kcol")], [R("bm")])
         ts(T.wcol[:, 0:1], T.rmask[:, 0:1], 256.0, T.rmask[:, 1:2], OP.mult, OP.add, [R("rmask")], [R("wcol")])
-        ts(T.bev[:], T.i5[:], T.even[:, 0:1], None, OP.mult, None, [R("i5"), R("even")], [R("bev")])
-        ts(T.base[:], T.bm[:], T.wcol[:, 0:1], None, OP.mult, None, [R("bm"), R("wcol")], [R("base")])
-        batch("v", [(lambda b=b: V.tensor_scalar(T.iot[:, b * 256:(b + 1) * 256], T.il[:], T.odd[:, 0:1], T.bev[:, b:b + 1], OP.mult, OP.add),
-                     [R("il"), R("odd"), R("bev")], [R("iot", b * 256, (b + 1) * 256)]) for b in range(8)])
-        batch("s", [(lambda p=p: S.activation(T.zm[:, p:Z:16], T.zeb[:], COPY, scale=T.rmask[:, p:p + 1]),
-                     [R("zeb"), R("rmask")], [R("zm")]) for p in range(16)], acc=True)
-        batch("s", [(lambda r=r: S.activation(T.dd[:, r * 128 + r:(r + 1) * 128:16], T.base[:, r:128:16], COPY),
-                     [R("base")], [R("dd")]) for r in range(16)], acc=True)
-        for nm in ("na", "nb"):
-            op("s", lambda: S.activation(T[nm][:, Z:WZ], T.il[:], IDENT, scale=0.0, bias=8.0), [R("il")], [R(nm, Z, WZ)])
-        addup(*FP, True)
-        addup(*FQ, True)
-        for nm, dst, o in (("sb", "lb", 2048), ("sa", "la", 2560)):
-            items = []
-            for i in range(6):
-                buf, a = ("ph", zone * 128) if i == rank else ("lpi", i * 128)
-                items.append((lambda i=i, buf=buf, a=a: PE.matmul(T.ps[:, o:o + 128], T[nm][:, i * 128:(i + 1) * 128], T[buf][:, a:a + 128], i == 0, i == 5),
-                              [R(nm, i * 128, (i + 1) * 128), R(buf, a, a + 128)], [R("ps", o, o + 128)]))
-            batch("t", items, acc=True)
-            cp(T[dst][:], T.ps[:, o:o + 128], [R("ps", o, o + 128)], [R(dst)])
-        send(B, "rlb", T.lb[:], T.lb[:], [R("lb")])
-        if l in hasQ:
-            near_pieces(qsrc, "lnq", solvers, Z, all_es)
-        addup(*FP, False)
-        addup(*NP, True)
-        addup(*FQ, False)
-
-        def scat(i):
-            cp(T.inv[:, 0:Z].indirect(T.lb[:, i * 32:(i + 1) * 32]), T.iot[:, i * 512:(i + 1) * 512], [R("lb"), R("iot")], [R("inv")])
-        scat(0)
-        far_p()
-        scat(1)
-        scat(2)
-        far_q()
-        fill("bz", 0.0, 0, 128)
         ts(T.bz[:, 0:128:2], T.bm[:, 0:128:2], 8.0, None, OP.mult, None, [R("bm")], [R("bz")])
-        fill("fi", 255)
-        scat(3)
-        addup(*NP, False)
-        for b in range(2):
-            o, c0 = 2048 + 512 * b, 512 * b
-            op("s", lambda: S.activation(T.nsp[:, c0:c0 + 512], T.ps[:, o:o + 512], COPY, scale=-1.0), [R("ps", o, o + 512)], [R("nsp", c0, c0 + 512)])
-        send(B, "rrnp", T.rnp[:], T.nsp[:], [R("nsp")])
-        for b in range(4):
-            c0, c1 = 512 * b, 512 * b + 512
-            op("t", lambda: PE.matmul(T.ps[:, c0:c1], T.bz[:], T.zm[:, c0:c1], True, True), [R("bz"), R("zm", c0, c1)], [R("ps", c0, c1)])
-            tt(T.invz[:, c0:c1], T.inv[:, c0:c1], T.ps[:, c0:c1], OP.max, [R("inv", c0, c1), R("ps", c0, c1)], [R("invz", c0, c1)])
+        ts(T.base[:], T.bm[:], T.wcol[:, 0:1], None, OP.mult, None, [R("bm"), R("wcol")], [R("base")])
+        fill("dd", 0.0, 0, Z)
 
-        def rows(src, h):
-            c0, c1, o = h * H, (h + 1) * H, 2048 + 512 * h
+        def list_weights():
+            batch("s", [(lambda r=r: S.activation(T.dd[:, r * 128 + r:(r + 1) * 128:16], T.base[:, r:128:16], COPY),
+                         [R("base")], [R("dd", r * 128, (r + 1) * 128)]) for r in range(16)])
+        if WF:
+            spread_zero(CFG["zm_early"], 16)
+            if CFG["dd_early"]:
+                list_weights()
+        add_landed(FP, CFG["fpn"])
+        if QI:
+            add_landed(FQ, CFG["fqn"])
+        near_x(nears[:CFG["xn"]])
+        for z in picks:
+            gather("s", z)
+        todo, pieces = list(mine), [i for i, f in enumerate(FAR) if (f[0] == "q" if WF else f[0] == "p" or QI)]
+        if WF:
+            for b in range(4):
+                c0, c1 = 512 * b, 512 * b + 512
+                if b < CFG["p_early"]:
+                    far_p(b)
+                cp(T.wb[:, c0:c1], T.ps[:, c0:c1], [R("ps", c0, c1)], [R("wb", c0, c1)], CFG["pev"][b])
+            for b in range(4):
+                pick(CFG["ppk"][b], "vc", 512 * b, "wb", 0, Z, "lb", 256 + 32 * b, 512)
+        for n in CFG["weave"] + ((0,) * 8 if QI else ()):
+            if not pieces:
+                break
+            scat(todo[:n])
+            todo = todo[n:]
+            far_piece(pieces.pop(0))
+        near_x(nears[CFG["xn"]:])
+        if l in hasQ and data:
+            for z in picks:
+                hand(z, qsrc, "lnq")
+        scat(todo)
+        if not WF:
+            spread_zero(CFG["zm_early"], 16)
+        if not (WF and CFG["dd_early"]):
+            list_weights()
+        seq = [t for t in CFG["merge"] if (SPLIT or t != "inw") and (mine or t != "inv")]
+        for src in seq:
+            for b in range(4):
+                c0, c1, wt = 512 * b, 512 * b + 512, "bz" if src == "zm" else "idb"
+                o = Z * WF + c0
+                batch("t", [(lambda: PE.matmul(T.ps[:, o:o + 512], T[wt][:], T[src][:, c0:c1], src == seq[0], src == seq[-1]),
+                             [R(wt), R(src, c0, c1)], [R("ps", o, o + 512)])], acc=True)
+                if src == seq[-1]:
+                    cp(T.invz[:, c0:c1], T.ps[:, o:o + 512], [R("ps", o, o + 512)], [R("invz", c0, c1)], "vs"[b % 2])
+
+        def rows(src, h, bank=4):
+            c0, c1, o = h * H, (h + 1) * H, 512 * (bank + h)
             batch("t", [(lambda r=r: PE.matmul(T.ps[:, o:o + 64], T.dd[:, r * 128:(r + 1) * 128], T[src][:, c0 + r:c1:16], r == 0, r == 15),
                          [R("dd"), R(src, c0, c1)], [R("ps", o, o + 64)]) for r in range(16)], acc=True)
 
-        def tab(lst, h):
-            o = 2048 + 512 * h
-            cp(T[lst][:, h * 64:(h + 1) * 64], T.ps[:, o:o + 64], [R("ps", o, o + 64)], [R(lst, h * 64, (h + 1) * 64)])
+        def tab(lst, h, bank=4):
+            o = 512 * (bank + h)
+            ts(T[lst][:, h * 64:(h + 1) * 64], T.ps[:, o:o + 64], float(Z), None, OP.min, None, [R("ps", o, o + 64)], [R(lst, h * 64, (h + 1) * 64)])
 
-        def give(lst):
-            send(B, "r" + lst, T[lst][:], T[lst][:], [R(lst)])
-
-        for t in range(7):
+        made = ["nl%d" % t for t in range(6)] + [None, "lm"]
+        for t in range(8):
             w, old = ("na", "nb")[t % 2], ("nb", "na")[t % 2]
-            src, ww, lst = ("invz", Z, "la") if t == 0 else (old, WZ, "nl%d" % (t - 1))
+            src, ww, lst = ("invz", Z, "lb") if t == 0 else (old, WZ, made[t - 1] or "li")
             for h in range(2):
-                if h == 1 and t > 0:
+                if h == 1 and t > 0 and made[t - 1]:
                     tab(lst, 1)
-                    give(lst)
+                    give(lst, 1 if lst in EARLY else None)
                 for e, c in (("v", h * H), ("s", h * H + 512)):
-                    pick(e, w, c, src, 0, ww, lst, c // 16, 512)
-                rows(w, h)
-            tab("nl%d" % t, 0)
-        tab("nl6", 1)
-        give("nl6")
-        for h in range(2):
-            rows("invz", h)
-            tab("li", h)
-        give("li")
-        for c0, c1 in CH:
-            ts(T.fi[:, c0:c1], T.v7[:, c0:c1], 255, None, OP.bitwise_and, None, [R("v7", c0, c1)], [R("fi", c0, c1)])
-        for c0, c1 in CH:
-            ts(T.yo[:, c0:c1], T.fi[:, 0:WZ].indirect(T.li[:, c0 // 16:c1 // 16]), -1.0, 255.0, OP.mult, OP.add,
-               [R("fi"), R("li", c0 // 16, c1 // 16)], [R("yo", c0, c1)])
-            store(c0, c1)
+                    pick(e, w, c, src, 0, ww, lst, c // 16 + 128 * (t == 0), 512)
+                if made[t]:
+                    rows(w, h)
+            if made[t]:
+                tab(made[t], 0)
+                if made[t] in EARLY:
+                    give(made[t], 0)
+            if WF and CFG["p_early"] < t <= 4:
+                far_p(t - 1)
+            if t == 2:
+                for h in range(2):
+                    rows("invz", h, 6)
+            if t == 3:
+                for h in range(2):
+                    tab("li", h, 6)
+                give("li")
+        tab("lm", 1)
+        give("lm")
+        if CFG["fold"]:
+            for i in range(len(TAIL)):
+                round_down(i, 1, CFG["i1"][i], CFG["i2"][i])
+                rest(i, 1)
+        else:
+            bank = [(T.ps[:, 512 * i:512 * i + c1 - c0], R("ps", 512 * i, 512 * i + 512)) for i, (c0, c1) in enumerate(TAIL)]
+            ts(T.idf[:], T.i1[:], 0, None, OP.is_equal, None, [R("i1")], [R("idf")])
+            ts(T.idh[:], T.i1[:], 0, None, OP.is_equal, None, [R("i1")], [R("idh")])
+            fill("wa", 0.0)
+            for i in CFG["self"]:
+                last_step(i, "s")
+                last_step(i, "v")
+            for src in ("p1", "rfp", "raw"):
+                for i in CFG["iorder"]:
+                    c0, c1 = TAIL[i]
+                    terms = ["p1"] + ["rfp"] * WF + ["raw"] * (CFG["i0"][i] == "t")
+                    wt = "idh" if src == "rfp" else "idf"
+                    if src in terms:
+                        batch("t", [(lambda: PE.matmul(bank[i][0], T[wt][:], T[src][:, c0:c1], src == terms[0], src == terms[-1]),
+                                     [R(wt), R(src, c0, c1)], [bank[i][1]])], acc=True)
+
+            def step(i, n):
+                c0, c1 = TAIL[i]
+                if n == 0 and CFG["i0"][i] == "v":
+                    tt(bank[i][0], bank[i][0], T.raw[:, c0:c1], OP.add, [bank[i][1], R("raw", c0, c1)], [bank[i][1]])
+                elif n == 1:
+                    affine(CFG["i1"][i], T.qq[:, c0:c1], bank[i][0], (1 + 2.0 ** -20) / 256, 2.0 ** 23 - 0.5, [bank[i][1]], [R("qq", c0, c1)])
+                elif n == 2:
+                    affine(CFG["i2"][i], T.pb[:, c0:c1], T.qq[:, c0:c1], -256.0, 2.0 ** 31, [R("qq", c0, c1)], [R("pb", c0, c1)])
+                elif n == 3:
+                    tt(T.yo[:, c0:c1], bank[i][0], T.pb[:, c0:c1], OP.add, [bank[i][1], R("pb", c0, c1)], [R("yo", c0, c1)])
+                    store(c0, c1)
+            lag = CFG["lag"]
+            for i, n in sorted(((i, n) for i in range(len(TAIL)) for n in range(4)), key=lambda e: (e[0] + lag[e[1]], -e[1])):
+                step(i, n)
     else:
-        if l in hasQ:
-            near_pieces(qsrc, "lnq", solvers, Z, all_es)
-        addup(*FP, True)
-        addup(*FQ, True)
-        addup(*NP, True, plus=False)
-        addup(*FP, False)
-        addup(near, qsrc, "lnq", hasQ, 6, True, 1)
-        addup(*FQ, False)
-        far_p()
-        far_q()
-        fill("v7", -1)
-        fill("wa", 0.0)
-        fill("wb", 0.0)
-        addup(*NP, False, plus=False)
-        addup(near, qsrc, "lnq", hasQ, 6, False, 1)
-        addup(near, qsrc, "lnq", hasQ, 2, True, 0)
-        addup(near, qsrc, "lnq", hasQ, 2, False, 0)
+        FQ = (fz, qsrc, "lfq", hasQ, 4)
+        NP, NQ_ = (zone, "xs", "lnp", hasP, 0), (zone, qsrc, "lnq", hasQ, 4)
+        plast = None if WF else "rfp"
+        addup(*NP, [l], last=plast)
+        if not QI:
+            addup(*FQ, [l], range(3))
+        choose()
+        if not QI:
+            addup(*FQ, [l], [3])
+        if CFG["lb_first"]:
+            send(C[rank + 1], "rpi", T.lb[:, 0:LW], T.lb[:, 0:LW], [R("lb")], on_es)
+        near_x()
+        if not CFG["lb_first"]:
+            send(C[rank + 1], "rpi", T.lb[:, 0:LW], T.lb[:, 0:LW], [R("lb")], off_es)
+        for z in picks:
+            gather("s", z)
+        order = arrival("lnq")
+        for s in order:
+            if at_w(s, l):
+                cp(T.lq[:, s * 128:(s + 1) * 128], T.lpi[:, local[s] * 256 + zone // 2 * 128:local[s] * 256 + zone // 2 * 128 + 128], [R("lpi")], [R("lq", s * 128, (s + 1) * 128)])
 
-        def settle(dst, h, add, a, bank, o):
-            for b in range(2):
-                p, c0, d = (bank + b) * 512, h * H + 512 * b, a + 512 * b
-                tt(T[dst][:, c0:c0 + 512], T.ps[:, p:p + 512], T[add][:, d:d + 512], o,
-                   [R("ps", p, p + 512), R(add, d, d + 512)], [R(dst, c0, c0 + 512)])
+        def pick_landed(e):
+            for s in order:
+                w = at_w(s, l) or ""
+                for h in range(len(w)):
+                    if w[h] == e:
+                        n = Z // len(w)
+                        pick(e, "lnq", s * Z + h * n, "lnp", s * Z, (s + 1) * Z, "lq", s * 128 + h * n // 16, n)
+        pick_landed("s")
+        for s in arrival("lnp")[:CFG["np_before"]]:
+            addup(*NP, [s], last=plast)
+        if not QI:
+            add_landed(FQ, CFG["fqn"])
+        if l in hasQ and nears[0] in picks:
+            hand(nears[0], qsrc, "lnq")
+        todo, pieces = list(mine), [i for i, f in enumerate(FAR) if f[0] == "q"]
+        for n in () if QI else CFG["wweave"]:
+            scat(todo[:n])
+            if todo and not todo[n:]:
+                send(C[rank + 1], "rinw", T.inw[:], T.inv[:], [R("inv")])
+            todo = todo[n:]
+            far_piece(pieces.pop(0))
+        if todo:
+            scat(todo)
+            send(C[rank + 1], "rinw", T.inw[:], T.inv[:], [R("inv")])
+        pick_landed("v")
+        for n, s in enumerate(arrival("lnp")):
+            if n == CFG["nq_own"]:
+                addup(*NQ_, [l], last="rfq")
+            if n >= CFG["np_before"]:
+                addup(*NP, [s], last=plast)
+        if CFG["nq_own"] == 3:
+            addup(*NQ_, [l], last="rfq")
+        for s in order[:CFG["nq_before"]]:
+            addup(*NQ_, [s], last="rfq")
+        for i, (kind, c0, c1, via) in sorted(enumerate(FAR), key=lambda e: e[1][3] is not None):
+            if kind == "p" and not WF:
+                addup(*NP, ["rfp"], range(c0 // 512, c1 // 512), "rfp")
+        for b, e in ((1, "v"), (2, "s"), (3, "v"), (0, "s")):
+            cp(T.p1[:, 512 * b:512 * b + 512], T.ps[:, 512 * b:512 * b + 512], [R("ps", 512 * b, 512 * b + 512)], [R("p1", 512 * b, 512 * b + 512)], e)
+        for b, e in ((2, "v"), (3, "s"), (0, "v"), (1, "s")):
+            pick(e, "pb", 512 * b, "p1", 0, Z, "lb", 32 * b, 512)
+        for s in order[CFG["nq_before"]:]:
+            addup(*NQ_, [s], last="rfq")
+        for i in CFG["qorder"]:
+            kind, c0, c1, via = [f for f in FAR if f[0] == "q"][i]
+            if kind == "q":
+                addup(*NQ_, ["rfq"], range(c0 // 512, c1 // 512), "rfq")
+                for c in range(c0, c1, 512):
+                    tt(T.wa[:, c:c + 512], T.ps[:, Z + c:Z + c + 512], T.pb[:, c:c + 512], OP.subtract,
+                       [R("ps", Z + c, Z + c + 512), R("pb", c, c + 512)], [R("wa", c, c + 512)])
+                    cp(T.vc[:, c:c + 512], T.wa[:, c:c + 512], [R("wa", c, c + 512)], [R("vc", c, c + 512)], "s")
 
-        def comb(dst, win, ww, lst, add, c0, c1, o):
-            tt(T[dst][:, c0:c1], T[win][:, 0:ww].indirect(T[lst][:, c0 // 16:c1 // 16]), T[add][:, c0:c1], o,
-               [R(win, 0, ww), R(lst), R(add, c0, c1)], [R(dst, c0, c1)])
-
-        settle("p1", 1, "rfp", H, 4, OP.subtract)
-        settle("q1", 1, "rfq", H, 6, OP.add)
-        for c0, c1 in ((0, 512), (512, H)):
-            tt(T.p1[:, c0:c1], T.rnp[:, c0:c1], T.rfp[:, c0:c1], OP.subtract, [R("rnp", c0, c1), R("rfp", c0, c1)], [R("p1", c0, c1)])
-        for t in range(7):
-            w, old = ("wa", "wb")[t % 2], ("wb", "wa")[t % 2]
-            for c0, c1 in ((H, Z), (0, H)):
-                if t == 0:
-                    if c0 == 0:
-                        settle("q1", 0, "rfq", 0, 2, OP.add)
-                    comb(w, "p1", Z, "lb", "q1", c0, c1, OP.add)
-                else:
-                    comb(w, old, WZ, "nl%d" % (t - 1), "vc", c0, c1, OP.add)
-                op("s", lambda: S.activation(T.vc[:, c0:c1], T[w][:, c0:c1], IDENT, bias=-1.0 if t == 6 else 0.0), [R(w, c0, c1)], [R("vc", c0, c1)])
-        for c, (c0, c1) in enumerate(CH):
-            comb("v7", "wa", WZ, "nl6", "vc", c0, c1, OP.add)
-            send(C[rank - 1], "rv%d" % c, T.v7[:, c0:c1], T.v7[:, c0:c1], [R("v7", c0, c1)])
-        hs = ((0, H), (H, Z))
-        for c0, c1 in hs:
-            comb("fi", "v7", WZ, "li", "p1", c0, c1, OP.subtract)
-        for c0, c1 in hs:
-            ts(T.fj[:, c0:c1], T.fi[:, c0:c1], 255, None, OP.bitwise_and, None, [R("fi", c0, c1)], [R("fj", c0, c1)])
-            cp(T.yo[:, c0:c1], T.fj[:, c0:c1], [R("fj", c0, c1)], [R("yo", c0, c1)])
-            store(c0, c1)
+        if not CFG["fold"]:
+            send(C[rank + 1], "rp1", T.p1[:], T.p1[:], [R("p1")])
+        for t in range(6):
+            old, w = ("wa", "wb")[t % 2], ("wb", "wa")[t % 2]
+            for c0, c1 in ((0, H), (H, Z)):
+                comb(w, old, "nl%d" % t, "vc", c0, c1)
+                if t < 5:
+                    cp(T.vc[:, c0:c1], T[w][:, c0:c1], [R(w, c0, c1)], [R("vc", c0, c1)], "s")
+                elif CFG["self"]:
+                    send(C[rank + 1], "rwa%d" % (c0 // H), T.wa[:, c0:c1], T.wa[:, c0:c1], [R("wa", c0, c1)])
+        for i in range(len(TAIL)):
+            last_step(i, "s")
+        for i, (c0, c1) in enumerate(TAIL):
+            last_step(i, "v")
+            if i in CFG["self"]:
+                continue
+            send_all([([rank + 1], "rz%d" % i, T.raw[:, c0:c1], [T.raw[:, c0:c1], T.p1[:, c0:c1]][:1 + CFG["fold"]], all_es)], [R("raw", c0, c1), R("p1", c0, c1)])
+        for i in WFLOAT:
+            round_down(i, -1)
+        for i in range(len(TAIL)):
+            if i not in WFLOAT:
+                by_bits(i, -1)
+        for i in WFLOAT:
+            rest(i, -1)
     finish(sent[0])

from concourse.bass import DstId, RemoteDMATransfer
from concourse.mybir import AluOpType, ActivationFunctionType

OP = AluOpType
COPY = ActivationFunctionType.Copy
IDENT = ActivationFunctionType.Identity
Z = 2048
H = 1024
WZ = Z + 16
NL = 87
LISTS = ["li", "lm"] + ["nl%d" % t for t in range(6)]
EARLY = ("nl0", "nl1")
FAR = (("p", 0, 512, 0), ("p", 512, H, None), ("p", H, 1536, None), ("p", 1536, Z, None),
       ("q", 0, 512, 0), ("q", 512, H, 0), ("q", H, 1536, None), ("q", 1536, Z, 0))
TAIL = ((0, 256), (256, 768), (768, 1280), (1280, 1792), (1792, 2048))
WFLOAT, IFLOAT = (0, 1, 2, 4), (0, 1, 2, 3, 4)
LIFT = 2.0 ** 19
CFG = {"ungated": (2, 2), "gate": 0, "arr": {"lfp": "JWM", "lfq": "MJW", "lnp": "WMJ", "lnq": "WMJ"}, "fpn": 0, "fqn": 2, "nq_own": 3, "relay_on": "", "i1": "sssss", "i2": "ssvsv", "lane": {}, "xn": 2, "fold": 0, "atw": {"W": "s", "I": "s", "J": "v"}, "fq_own": 4, "sa_at": 0, "lb_first": False, "wweave": (8, 0, 0, 0), "zm_early": 0, "sb_at": -1, "ddv": 0, "nq_before": 1, "weave": (0, 0, 0, 0), "merge": ("zm", "inw", "inv"), "xnear_first": True, "nq": 2, "wearly": True, "lnq_first": True, "split": 3, "s0": 2, "iq_first": 0,
       }
PAIR = (0, 2, 1, 3)
CFG.update(x_es=("all", "all"), p_early=1, dd_early=0, wf=False, pev="svsv", ppk="svsv", i0="vvvvv", lag=(0, 0.1, 0.2, 1.05), self=(), iorder=(0, 1, 2, 3, 4), qi=False, xq=0, np_before=0, dm_early=(0, 0), marks=0, qorder=(0, 1, 2, 3), fold=0, i2="sssss", pi2=0, wweave=(3, 0, 0, 0), lb_first=False, nq=1, split=3, nq_own=2, relay_on="q")

SCRATCH = {"ps": ("psum", [128, 4096], "float32")}
for _names, _cols, _dt in (
        ("xs qs lfp lfq lnp lnq", 4 * Z, "bfloat16"),
        ("zm yo dd inv inw invz", Z, "bfloat16"), ("iot", Z, "bfloat16"),
        ("dm", 512, "bfloat16"), ("zeb bm bz base idb", 128, "bfloat16"), ("na nb", WZ, "bfloat16"), ("il", 256, "bfloat16"),
        ("pin", 512, "int32"), ("losti", 2, "int32"), ("zin i1 i3", 128, "int32"), ("i2 i2b", 16, "int32"),
        ("i4 i4b i4c", 4, "int32"), ("i5", 8, "int32"), ("fi fj", Z, "int32"),
        ("lp lq", 512, "uint16"), (" ".join(LISTS) + "", 128, "uint16"), ("lb", 384, "uint16"),
        ("ph", 512, "float16"), ("sa sb", 768, "float16"), ("lpi", 1536, "float16"), ("idh", 128, "float16"),
        ("rfp rfq fsp fsq", Z, "float16"),
        ("lostf", 2, "float32"), ("idf", 128, "float32"), ("kcol odd even wcol", 4, "float32"), ("rmask", 16, "float32"), ("ea eb ms mn bev", 8, "float32"),
        ("p1 pb vc raw qq", Z, "float32"), ("wa wb", WZ, "float32")):
    for _n in _names.split():
        SCRATCH[_n] = ("sbuf", [128, _cols], _dt)
SEMAPHORES = (["l%d" % i for i in range(NL)] + ["snt", "rpi", "rinw", "rp1", "rwa0", "rwa1", "rlf"]
              + ["r%s%d" % (b, s) for b in ("lnp", "lnq") for s in range(4)]
              + ["r%s%d%d" % (b, s, h) for b in ("lfp", "lfq") for s in range(4) for h in range(2)]
              + ["rfar%d" % i for i in range(len(FAR))] + ["rrelay%d" % i for i in range(len(FAR))]
              + ["rz%d" % i for i in range(len(TAIL))] + ["r" + n for n in LISTS] + ["rh" + n for n in EARLY])


def tracker(g, T):
    E = {"g": g, "v": g.vector, "s": g.scalar, "t": g.tensor, "y": g.sync}
    known = {e: {} for e in E}
    count, waited, recs = {}, {}, {}
    free = ["l%d" % i for i in range(NL)]
    own = {e: [] for e in E}

    def wait(e, tok):
        sem, val, snap = tok
        k = known[e]
        if k.get(sem, 0) >= val:
            return
        E[e].wait_ge(T.sem[sem], val)
        waited[sem] = max(waited.get(sem, 0), val)
        k[sem] = val
        for s, n in snap.items():
            if k.get(s, 0) < n:
                k[s] = n

    def span(r):
        b, a, z = r
        return (b, a // 512 * 512, -(-z // 512) * 512) if b == "ps" else (b, a, z)

    def conflicts(who, reads, writes, acc):
        out = []
        for r in reads:
            b, a, z = span(r)
            for (x, y, kind, w, tok) in recs.get(b, []):
                if x < z and a < y and (kind == "w" or (b == "ps" and w != who)):
                    out.append(tok)
        for r in writes:
            b, a, z = span(r)
            for (x, y, kind, w, tok) in recs.get(b, []):
                if x < z and a < y and not (w == who and (kind == "r" or acc)):
                    out.append(tok)
        return out

    def note(reads, writes, who, tok):
        for r in writes:
            b, a, z = span(r)
            recs[b] = [q for q in recs.get(b, []) if not (a <= q[0] and q[1] <= z and q[4] is not tok)] + [(a, z, "w", who, tok)]
        for r in reads:
            b, a, z = span(r)
            recs.setdefault(b, []).append((a, z, "r", who, tok))

    def batch(e, items, dma=False, acc=False):
        who = "dma" if dma else e
        ins = []
        for fn, reads, writes in items:
            for t in sorted(conflicts(who, reads, writes, acc), key=lambda t: -len(t[2])):
                wait(e, t)
            ins.append(fn())
        done = [s for s in own[e] if known[e].get(s, 0) == count[s]]
        if not done:
            done = [free.pop(0)]
            own[e].append(done[0])
            count[done[0]] = 0
        sem = done[0]
        for i in ins:
            i.then_inc(T.sem[sem], 16 if dma else 1)
            count[sem] += 16 if dma else 1
        tok = (sem, count[sem], dict(known[e]))
        for fn, reads, writes in items:
            note(reads, writes, who, tok)

    def op(e, fn, reads, writes, dma=False):
        batch(e, [(fn, reads, writes)], dma)

    def landing(b, a, z, sem, val):
        count[sem] = val
        note([], [(b, a, z)], "remote", (sem, val, {}))

    def reading(e, reads):
        for t in conflicts(e, reads, [], False):
            wait(e, t)

    def finish(sent):
        count["snt"] = sent
        for s, n in count.items():
            if waited.get(s, 0) < n:
                g.wait_ge(T.sem[s], n)

    return op, batch, landing, reading, finish


def bits(es):
    return sum(1 << e for e in es)


def relay_of(core, j, T, topo):
    cs = topo.cores_of(core)
    same = [c for c in cs if T.rank_of(c) is not None and topo.die(c) == topo.die(core)]
    free = [c for c in cs if T.rank_of(c) is None and topo.die(c) != topo.die(core)]
    return free[same.index(core) + j]


def far_solver(core, C, topo):
    here = [c for c in C if topo.chip(c) == topo.chip(core)]
    zs = [z for z in range(4) if C[2 * z] not in here]
    return C[2 * zs[here.index(core) // 2]]


def relay_engines(c, to, relay, topo):
    return [e for e in topo.engines(c, relay) if e not in topo.engines(c, to)]


def hop_lanes(kind, all_es, off_es):
    if CFG["relay_on"] == "all":
        return all_es
    return [e for e in all_es if e not in off_es] if kind in CFG["relay_on"] else off_es


def rank_program(g, core, T, topo):
    rank = T.rank_of(core)
    C = list(T.cores)
    if rank is None:
        n = 0
        for c in C[0::2]:
            for i, (kind, c0, c1, via) in enumerate(FAR):
                if topo.chip(c) == topo.chip(core) and via is not None and relay_of(c, via, T, topo) == core:
                    to = far_solver(c, C, topo)
                    a = topo.addr(C[C.index(to) + 1] if CFG["wf"] and kind == "p" else to)
                    g.wait_ge(T.sem["rrelay%d" % i], len(hop_lanes(kind, topo.engines(c, core), topo.engines(c, to))))
                    g.remote_dma(out_ap=T["rf" + kind][:, c0:c1], in_ap=T["fs" + kind][:, c0:c1], remote_sem=T.sem["rfar%d" % i],
                                 local_sem=T.sem["snt"], pid=a[1], routing_id=a[0], dma_engine_mask=topo.mask(core, to))
                    n += len(topo.engines(core, to))
        if n:
            g.wait_ge(T.sem["snt"], n)
        return
    V, S, PE = g.vector, g.scalar, g.tensor
    op, batch, landing, reading, finish = tracker(g, T)
    local = [r for r in range(8) if topo.chip(C[r]) == topo.chip(core)]
    l = local.index(rank)
    near = sorted({r // 2 for r in local})
    far = [z for z in range(4) if z not in near]
    isW = rank % 2 == 0
    zone = rank // 2
    data = rank < 6
    hasP = [s for s in range(4) if local[s] != 7]
    hasQ = [s for s in range(4) if local[s] != 6]
    away = [r for r in range(8) if r not in local]
    all_es = topo.engines(core, C[local[l ^ 1]])
    off_es = topo.engines(core, C[away[0]])
    on_es = [e for e in all_es if e not in off_es]
    SPLIT = CFG["split"]
    mine = list(range(8 - SPLIT, 8) if isW else range(8 - SPLIT))
    NQ = CFG["nq"]
    QW = Z // NQ
    sent = [0]

    def R(b, a=0, z=None):
        return (b, a, SCRATCH[b][1][1] if z is None else z)

    def send(to, sem, dst, src, reads, es=None):
        reading("g", reads)
        a = topo.addr(to)
        es = topo.engines(core, to) if es is None else es
        g.remote_dma(out_ap=dst, in_ap=src, remote_sem=T.sem[sem], local_sem=T.sem["snt"], pid=a[1], routing_id=a[0],
                     dma_engine_mask=bits(es))
        sent[0] += len(es)

    def send_all(parts, reads):
        reading("g", reads)
        trs = []
        for rs, sem, dst, srcs, es in parts:
            ids = [DstId(rid=topo.addr(C[r])[0], pnc=topo.addr(C[r])[1]) for r in rs]
            trs.append(RemoteDMATransfer(dst_ids=ids, dma_engine_mask=bits(es), remote_sem=T.sem[sem],
                                         srcs=srcs, dsts=[dst] * len(rs), alu_op=1 if len(srcs) > 1 else 0))
            sent[0] += len(es)
        g.remote_dma_fused(trs, local_sem=T.sem["snt"])

    def at_w(s, w):
        return local[s] < 6 and s != w and CFG["atw"].get("W" if s % 2 == 0 else "I" if s == w + 1 else "J")

    full = len(all_es)
    WF = CFG["wf"]
    LW = 384 if WF else 256
    x_es = [{"on": on_es, "off": off_es, "all": all_es}[k] for k in CFG["x_es"]]

    def list_es(n):
        return on_es if WF else all_es
    QI = CFG["qi"] or WF
    for i, (kind, c0, c1, via) in enumerate(FAR):
        if isW != (WF and kind == "p"):
            landing("rf" + kind, c0, c1, "rfar%d" % i, len(off_es))
    q_es = off_es if CFG["xq"] else all_es
    if isW != QI:
        for s in hasQ:
            if s != l:
                for h in range(NQ):
                    landing("lfq", s * Z + h * QW, s * Z + (h + 1) * QW, "rlfq%d%d" % (s, h), len(q_es) // 2 if s % 2 != l % 2 else len(q_es))
    def lanes(b, s, w):
        kind = CFG["lane"].get(b + ("W" if s % 2 == 0 else "I" if s == w + 1 else "J"), "on")
        return {"on": on_es, "off": off_es, "all": all_es}[kind]
    if isW:
        landing("lpi", 0, 1536, "rpi", 4 * (5 if data else 6))
        for s in range(4):
            if s != l:
                for b, who in (("lnp", hasP), ("lnq", hasQ)):
                    if s in who and not (b == "lnq" and at_w(s, l)):
                        landing(b, s * Z, (s + 1) * Z, "r%s%d" % (b, s), len(lanes(b, s, l)))
        for n in LISTS:
            if n in EARLY:
                landing(n, 0, 64, "rh" + n, len(list_es(n)))
                landing(n, 64, 128, "r" + n, len(list_es(n)))
            else:
                landing(n, 0, 128, "r" + n, len(list_es(n)))
    else:
        for s in hasP:
            if s != l:
                for h in range(2):
                    landing("lfp", s * Z + h * H, s * Z + (h + 1) * H, "rlfp%d%d" % (s, h), len(x_es[h]) // (1 if s % 2 else 2))
        landing("lb", 0, 384, "rpi", len(off_es))
        if not CFG["fold"]:
            landing("p1", 0, Z, "rp1", full)
        if SPLIT:
            landing("inw", 0, Z, "rinw", full)
        for i, (c0, c1) in enumerate(TAIL):
            if i not in CFG["self"]:
                landing("raw", c0, c1, "rz%d" % i, full)
        if CFG["self"]:
            for h in range(2):
                landing("wa", h * H, (h + 1) * H, "rwa%d" % h, full)

    def load(e, dst, src, w):
        q = g.sync if e == "y" else S
        op(e, lambda: q.dma_start(dst, src), [], [w], True)

    def loadx(e, z):
        load(e, T.xs[:, z * Z:(z + 1) * Z], T.x[:, z * Z:(z + 1) * Z], R("xs", z * Z, (z + 1) * Z))
    fars = sorted(far, key=lambda z: z == far[l // 2])
    nears = sorted(near, key=lambda z: (z == zone) == isW)
    if data:
        load("y", T.pin[:], T.pi[:], R("pin"))
    load("s", T.losti[:], T.lost[:], R("losti"))
    if not isW:
        load("s", T.zin[:], T.zero[:], R("zin"))
    loadx("y", fars[0])
    loadx("s", fars[1])
    ungated = CFG["ungated"][0 if isW else 1] if data else 2
    for z in nears[:ungated]:
        loadx("y", z)

    def iota(b, pattern, base, cm, **kw):
        op("g", lambda: g.iota(T[b][:], pattern, base, cm, **kw), [], [R(b)])
    iota("i1", [[-1, 128]], 0, 1)
    iota("i5", [[1, 8]], 0, 0)
    iota("i4", [[0, 4]], 0, 1)
    iota("il", [[1, 256]], 0, 0, allow_small_or_imprecise_dtypes=True)
    if not isW:
        iota("i2", [[-1, 16]], 16, 1)
        iota("i3", [[1, 8], [0, 16]], 0, 0)

    def ts(out, in0, s1, s2, op0, op1, reads, writes):
        a = (out, in0, s1, s2, op0) if op1 is None else (out, in0, s1, s2, op0, op1)
        op("v", lambda: V.tensor_scalar(*a), reads, writes)

    def tt(out, in0, in1, o, reads, writes):
        op("v", lambda: V.tensor_tensor(out, in0, in1, o), reads, writes)

    def cp(out, in_, reads, writes, e="v"):
        if e == "v":
            op("v", lambda: V.tensor_copy(out, in_), reads, writes)
        else:
            op("s", lambda: S.activation(out, in_, COPY), reads, writes)

    def fill(b, c, a=Z, z=WZ):
        op("v", lambda: V.memset(T[b][:, a:z], c), [], [(b, a, z)])

    def scaled(n, dst, idn, col):
        items = []
        for i in range(n):
            b, j = col(i)
            items.append((lambda i=i, b=b, j=j: V.tensor_scalar(T[dst][:, i * 128:(i + 1) * 128], T[idn][:], T[b][:, j:j + 1], None, OP.mult),
                          [R(idn), R(b)], [R(dst, i * 128, (i + 1) * 128)]))
        batch("v", items)

    def spread_zero(p0, p1):
        batch("s", [(lambda p=p: S.activation(T.zm[:, p:Z:16], T.zeb[:], COPY, scale=T.rmask[:, p:p + 1]),
                     [R("zeb"), R("rmask")], [R("zm")]) for p in range(p0, p1)])

    if 0 < SPLIT < 8:
        fill("inv", 0.0, 0, Z)
    ts(T.i4c[:], T.i4[:], 1, None, OP.bitwise_and, None, [R("i4")], [R("i4c")])
    if isW:
        ts(T.idh[:], T.i1[:], 0, None, OP.is_equal, None, [R("i1")], [R("idh")])
    cp(T.odd[:], T.i4c[:], [R("i4c")], [R("odd")])
    ts(T.even[:], T.i4c[:], 0, None, OP.is_equal, None, [R("i4c")], [R("even")])
    ts(T.idb[:], T.i1[:], 0, None, OP.is_equal, None, [R("i1")], [R("idb")])
    ts(T.bev[:], T.i5[:], T.even[:, 0:1], None, OP.mult, None, [R("i5"), R("even")], [R("bev")])
    if mine:
        batch("s", [(lambda b=b: S.activation(T.iot[:, b * 256:(b + 1) * 256], T.il[:], IDENT, scale=T.odd[:, 0:1], bias=T.bev[:, b:b + 1]),
                     [R("il"), R("odd"), R("bev")], [R("iot", b * 256, (b + 1) * 256)]) for b in mine])
    if isW:
        fill("wa", 0.0)
        fill("wb", 0.0)
    else:
        ts(T.i2b[:], T.i2[:], 15, None, OP.bitwise_and, None, [R("i2")], [R("i2b")])
        ts(T.i4b[:], T.i4[:], 4, None, OP.arith_shift_right, None, [R("i4")], [R("i4b")])
        ts(T.rmask[:], T.i2b[:], 0, None, OP.is_equal, None, [R("i2b")], [R("rmask")])
        cp(T.kcol[:], T.i4b[:], [R("i4b")], [R("kcol")])

    def marks():
        cp(T.lostf[:], T.losti[:], [R("losti")], [R("lostf")])
        ts(T.eb[:], T.i5[:], T.lostf[:, 1:2], None, OP.is_equal, None, [R("i5"), R("lostf")], [R("eb")])
        ts(T.ea[:], T.i5[:], T.lostf[:, 0:1], None, OP.is_equal, None, [R("i5"), R("lostf")], [R("ea")])
    if CFG["marks"]:
        marks()
    if data:
        for z0, z1 in ((0, 1), (1, 2), (2, 3), (3, 4)) if WF else ():
            cp(T.ph[:, PAIR[z0] * 128:PAIR[z0] * 128 + 128], T.pin[:, z0 * 128:z1 * 128], [R("pin")], [R("ph", PAIR[z0] * 128, PAIR[z0] * 128 + 128)])
        if not WF:
            cp(T.ph[:], T.pin[:], [R("pin")], [R("ph")])
        where = [(z, off_es[4 * i:4 * i + 4]) for i, z in enumerate(far)] + [(z, on_es[4 * i:4 * i + 4]) for i, z in enumerate(near)]
        for part in ((where[:2], where[2:]) if CFG["pi2"] else (where,)):
            send_all([([2 * z], "rpi", T.lpi[:, rank * 256:(rank + 1) * 256] if WF else T.lpi[:, rank * 256 + z // 2 * 128:rank * 256 + z // 2 * 128 + 128],
                       [T.ph[:, z % 2 * 256:z % 2 * 256 + 256] if WF else T.ph[:, z * 128:z * 128 + 128]], es) for z, es in part if 2 * z != rank], [R("ph")])
    if data:
        cp(T.lp[:], T.pin[:], [R("pin")], [R("lp")])
    if not CFG["marks"]:
        marks()
    tt(T.ms[:], T.ea[:], T.eb[:], OP.add, [R("ea"), R("eb")], [R("ms")])
    ts(T.mn[:], T.ms[:], -1.0, None, OP.add, None, [R("ms")], [R("mn")])

    def masks():
        batch("s", [(lambda i=i, r=r: S.activation(T.dm[:, i * 128:(i + 1) * 128], T.idb[:], COPY, scale=T.mn[:, r:r + 1]),
                     [R("idb"), R("mn")], [R("dm", i * 128, (i + 1) * 128)]) for i, r in enumerate(local) if r < 6])
    if CFG["dm_early"][0 if isW else 1]:
        masks()
    if not isW and CFG["zm_early"]:
        cp(T.zeb[:], T.zin[:], [R("zin")], [R("zeb")])
        spread_zero(0, CFG["zm_early"])

    def weights(h):
        if isW and CFG["sb_at"] == h:
            scaled(6, "sb", "idh", lambda i: ("eb", i))
        if isW and CFG["sa_at"] == h:
            scaled(6, "sa", "idh", lambda i: ("ea", i))
    weights(-1)

    def pick(e, dst, d0, src, s0, s1, lst, t0, n, bias=None):
        out, in_ = T[dst][:, d0:d0 + n], T[src][:, s0:s1].indirect(T[lst][:, t0:t0 + n // 16])
        rd, wr = [R(src, s0, s1), R(lst, t0, t0 + n // 16)], [R(dst, d0, d0 + n)]
        if e == "v":
            op("v", lambda: V.tensor_copy(out, in_), rd, wr)
        elif bias is None:
            op("s", lambda: S.activation(out, in_, COPY), rd, wr)
        else:
            op("s", lambda: S.activation(out, in_, IDENT, bias=bias), rd, wr)

    def gather(e, z, c0=0, c1=Z):
        if data:
            pick(e, "qs", z * Z + c0, "xs", z * Z, (z + 1) * Z, "lp", z * 128 + c0 // 16, c1 - c0)

    def adder(z, landb="lfq"):
        return local[2 * near.index(z) if z in near else 2 * far.index(z) + (landb == "lfp" or QI)]

    def hand(z, srcb, landb):
        if adder(z, landb) != rank:
            send(C[adder(z, landb)], "r%s%d" % (landb, l), T[landb][:, l * Z:(l + 1) * Z], T[srcb][:, z * Z:(z + 1) * Z],
                 [R(srcb, z * Z, (z + 1) * Z)], lanes(landb, l, local.index(adder(z))))

    qsrc = "qs" if data else "xs"

    def far_q(h):
        zs = [z for z in fars if adder(z) != rank]
        n = len(q_es) // len(zs)
        send_all([([adder(z)], "rlfq%d%d" % (l, h), T.lfq[:, l * Z + h * QW:l * Z + (h + 1) * QW],
                   [T[qsrc][:, z * Z + h * QW:z * Z + (h + 1) * QW]], q_es[i * n:(i + 1) * n]) for i, z in enumerate(zs)],
                 [R(qsrc, z * Z + h * QW, z * Z + (h + 1) * QW) for z in zs])

    for h in range(NQ):
        gather("v", fars[0], h * QW, (h + 1) * QW)
        gather("s", fars[1], h * QW, (h + 1) * QW)
        weights(h)
    if not CFG["dm_early"][0 if isW else 1]:
        masks()
    for z in nears[ungated:]:
        a = fars[0] * Z + CFG["gate"]
        op("y", lambda: g.sync.dma_start(T.xs[:, z * Z:(z + 1) * Z], T.x[:, z * Z:(z + 1) * Z]), [R("qs", a, a + 16)], [R("xs", z * Z, (z + 1) * Z)], True)
    if l in hasP:
        zs = [z for z in fars if adder(z, "lfp") != rank]
        for h in range(2):
            n = len(x_es[h]) // len(zs)
            send_all([([adder(z, "lfp")], "rlfp%d%d" % (l, h), T.lfp[:, l * Z + h * H:l * Z + (h + 1) * H],
                       [T.xs[:, z * Z + h * H:z * Z + (h + 1) * H]], x_es[h][i * n:(i + 1) * n]) for i, z in enumerate(zs)],
                     [R("xs", z * Z + h * H, z * Z + (h + 1) * H) for z in zs])
    handed = []

    def near_x(zs=nears):
        if l in hasP:
            for z in zs:
                if z not in handed:
                    hand(z, "xs", "lnp")
                    handed.append(z)
    near_x(nears[:CFG["xq"]])
    if l in hasQ:
        for h in range(NQ):
            far_q(h)

    def store(c0, c1):
        op("y", lambda: g.sync.dma_start(T.y[:, c0:c1], T.yo[:, c0:c1]), [R("yo", c0, c1)], [], True)

    def comb(dst, win, lst, add, c0, c1):
        tt(T[dst][:, c0:c1], T[win][:, 0:WZ].indirect(T[lst][:, c0 // 16:c1 // 16]), T[add][:, c0:c1], OP.add,
           [R(win, 0, WZ), R(lst, c0 // 16, c1 // 16), R(add, c0, c1)], [R(dst, c0, c1)])

    def last_step(i, e):
        c0, c1 = TAIL[i]
        if e == "s":
            pick("s", "vc", c0, "wa", 0, WZ, "li", c0 // 16, c1 - c0, LIFT)
        else:
            comb("raw", "wa", "lm", "vc", c0, c1)

    def affine(e, out, in_, scale, bias, reads, writes):
        if e == "v":
            ts(out, in_, scale, bias, OP.mult, OP.add, reads, writes)
        else:
            op("s", lambda: S.activation(out, in_, IDENT, scale=scale, bias=bias), reads, writes)

    def round_down(i, sign, e1="s", e2="s"):
        c0, c1 = TAIL[i]
        o = 512 * i
        affine(e1, T.qq[:, c0:c1], T.raw[:, c0:c1], (1 + sign * 2.0 ** -20) / 256, 2.0 ** 23 - 0.5, [R("raw", c0, c1)], [R("qq", c0, c1)])
        affine(e2, T.ps[:, o:o + c1 - c0], T.qq[:, c0:c1], -256.0 * sign, 2.0 ** 31 if sign > 0 else 256 - 2.0 ** 31,
               [R("qq", c0, c1)], [R("ps", o, o + 512)])

    def rest(i, sign):
        c0, c1 = TAIL[i]
        o = 512 * i
        tt(T.yo[:, c0:c1], T.ps[:, o:o + c1 - c0], T.raw[:, c0:c1], OP.add if sign > 0 else OP.subtract,
           [R("ps", o, o + 512), R("raw", c0, c1)], [R("yo", c0, c1)])
        store(c0, c1)

    def by_bits(i, sign):
        c0, c1 = TAIL[i]
        ts(T.fi[:, c0:c1], T.raw[:, c0:c1], float(sign), None, OP.mult, None, [R("raw", c0, c1)], [R("fi", c0, c1)])
        ts(T.fj[:, c0:c1], T.fi[:, c0:c1], 255, None, OP.bitwise_and, None, [R("fi", c0, c1)], [R("fj", c0, c1)])
        cp(T.yo[:, c0:c1], T.fj[:, c0:c1], [R("fj", c0, c1)], [R("yo", c0, c1)])
        store(c0, c1)

    def choose():
        items = []
        for nm, o, z in (("sb", 3584, zone), ("sa", 3712, zone), ("sb", 3840, fz))[:2 + WF]:
            for i in range(6):
                buf, a = ("ph", (PAIR[z] if WF else z) * 128) if i == rank else ("lpi", i * 256 + z // 2 * 128)
                items.append((lambda i=i, buf=buf, a=a, nm=nm, o=o: PE.matmul(T.ps[:, o:o + 128], T[nm][:, i * 128:(i + 1) * 128], T[buf][:, a:a + 128], i == 0, i == 5),
                              [R(nm, i * 128, (i + 1) * 128), R(buf, a, a + 128)], [R("ps", o, o + 128)]))
        batch("t", items, acc=True)
        cp(T.lb[:, 0:LW], T.ps[:, 3584:3584 + LW], [R("ps", 3584, 3968)], [R("lb")])

    def scat(bs):
        if bs:
            a, z = bs[0], bs[-1] + 1
            cp(T.inv[:, 0:Z].indirect(T.lb[:, a * 16:z * 16]), T.iot[:, a * 256:z * 256], [R("lb"), R("iot")], [R("inv")])

    fz = far[l // 2]
    to = far_solver(core, C, topo)
    others = [s for s in range(4) if s != l]
    picks = [z for z in nears if not at_w(l, local.index(adder(z)))]

    def arrival(landb):
        who = {"M": l ^ 1, "W": (l ^ 2) & 2, "J": (l ^ 2) | 1}
        return [who[c] for c in CFG["arr"][landb]]

    def add_landed(job, n, last=None):
        for s in arrival(job[2])[:n]:
            addup(*job, [s], last=last)
        addup(*job, arrival(job[2])[n:], last=last)

    def weight(s):
        return (T.dm[:, s * 128:(s + 1) * 128], R("dm", s * 128, (s + 1) * 128)) if local[s] < 6 else (T.idb[:], R("idb"))

    def addup(z, srcb, landb, who, bank, part, banks=range(4), last=None):
        seq = [s for s in [l] + arrival(landb) if s in who] + ([last] if last else [])
        for b in banks:
            items = []
            for n, s in enumerate(seq):
                if s in part:
                    wt, wr = (T.idh[:], R("idh")) if s == last else weight(s)
                    buf, a = (last, 512 * b) if s == last else (srcb, z * Z + 512 * b) if s == l else (landb, s * Z + 512 * b)
                    o = (bank + b) * 512
                    items.append((lambda o=o, wt=wt, buf=buf, a=a, n=n: PE.matmul(T.ps[:, o:o + 512], wt, T[buf][:, a:a + 512], n == 0, n == len(seq) - 1),
                                  [wr, R(buf, a, a + 512)], [R("ps", o, o + 512)]))
            if items:
                batch("t", items, acc=True)

    def far_piece(i):
        kind, c0, c1, via = FAR[i]
        src, o = "fs" + kind, Z * (kind == "q")
        for c in range(c0, c1, 512):
            if WF and kind == "q":
                tt(T[src][:, c:c + 512], T.ps[:, o + c:o + c + 512], T.vc[:, c:c + 512], OP.subtract,
                   [R("ps", o + c, o + c + 512), R("vc", c, c + 512)], [R(src, c, c + 512)])
            elif not WF:
                cp(T[src][:, c:c + 512], T.ps[:, o + c:o + c + 512], [R("ps", o + c, o + c + 512)], [R(src, c, c + 512)])
        if via is None:
            send(C[C.index(to) + 1] if WF and kind == "p" else to, "rfar%d" % i, T["rf" + kind][:, c0:c1], T[src][:, c0:c1], [R(src, c0, c1)])
        else:
            rl = relay_of(C[2 * zone], via, T, topo)
            send(rl, "rrelay%d" % i, T[src][:, c0:c1], T[src][:, c0:c1], [R(src, c0, c1)], hop_lanes(kind, all_es, off_es))

    def far_pieces(which):
        for i, f in enumerate(FAR):
            if f[0] == which:
                far_piece(i)

    if not isW:
        W = C[rank - 1]

        def give(lst, h=None):
            c0, c1 = (0, 128) if h is None else (64 * h, 64 * h + 64)
            send(W, ("rh" if h == 0 else "r") + lst, T[lst][:, c0:c1], T[lst][:, c0:c1], [R(lst, c0, c1)], list_es(lst))

        def far_p(b):
            c = 512 * b
            cp(T.fsp[:, c:c + 512], T.ps[:, c:c + 512], [R("ps", c, c + 512)], [R("fsp", c, c + 512)])
            for i, f in enumerate(FAR):
                if f[0] == "p" and c < f[2] <= c + 512:
                    far_piece(i)

        FP, FQ = (fz, "xs", "lfp", hasP, 0), (fz, qsrc, "lfq", hasQ, 4)
        if not data and l in hasQ:
            for z in nears:
                hand(z, qsrc, "lnq")
        addup(*FP, [l])
        if QI:
            addup(*FQ, [l])
        if not CFG["zm_early"]:
            cp(T.zeb[:], T.zin[:], [R("zin")], [R("zeb")])
        fill("bz", 0.0, 0, 128)
        for nm in ("na", "nb"):
            fill(nm, 8.0)
        ts(T.bm[:], T.i3[:], T.kcol[:, 0:1], None, OP.is_equal, None, [R("i3"), R("kcol")], [R("bm")])
        ts(T.wcol[:, 0:1], T.rmask[:, 0:1], 256.0, T.rmask[:, 1:2], OP.mult, OP.add, [R("rmask")], [R("wcol")])
        ts(T.bz[:, 0:128:2], T.bm[:, 0:128:2], 8.0, None, OP.mult, None, [R("bm")], [R("bz")])
        ts(T.base[:], T.bm[:], T.wcol[:, 0:1], None, OP.mult, None, [R("bm"), R("wcol")], [R("base")])
        fill("dd", 0.0, 0, Z)

        def list_weights():
            batch("s", [(lambda r=r: S.activation(T.dd[:, r * 128 + r:(r + 1) * 128:16], T.base[:, r:128:16], COPY),
                         [R("base")], [R("dd", r * 128, (r + 1) * 128)]) for r in range(16)])
        if WF:
            spread_zero(CFG["zm_early"], 16)
            if CFG["dd_early"]:
                list_weights()
        add_landed(FP, CFG["fpn"])
        if QI:
            add_landed(FQ, CFG["fqn"])
        near_x(nears[:CFG["xn"]])
        for z in picks:
            gather("s", z)
        todo, pieces = list(mine), [i for i, f in enumerate(FAR) if (f[0] == "q" if WF else f[0] == "p" or QI)]
        if WF:
            for b in range(4):
                c0, c1 = 512 * b, 512 * b + 512
                if b < CFG["p_early"]:
                    far_p(b)
                cp(T.wb[:, c0:c1], T.ps[:, c0:c1], [R("ps", c0, c1)], [R("wb", c0, c1)], CFG["pev"][b])
            for b in range(4):
                pick(CFG["ppk"][b], "vc", 512 * b, "wb", 0, Z, "lb", 256 + 32 * b, 512)
        for n in CFG["weave"] + ((0,) * 8 if QI else ()):
            if not pieces:
                break
            scat(todo[:n])
            todo = todo[n:]
            far_piece(pieces.pop(0))
        near_x(nears[CFG["xn"]:])
        if l in hasQ and data:
            for z in picks:
                hand(z, qsrc, "lnq")
        scat(todo)
        if not WF:
            spread_zero(CFG["zm_early"], 16)
        if not (WF and CFG["dd_early"]):
            list_weights()
        seq = [t for t in CFG["merge"] if (SPLIT or t != "inw") and (mine or t != "inv")]
        for src in seq:
            for b in range(4):
                c0, c1, wt = 512 * b, 512 * b + 512, "bz" if src == "zm" else "idb"
                o = Z * WF + c0
                batch("t", [(lambda: PE.matmul(T.ps[:, o:o + 512], T[wt][:], T[src][:, c0:c1], src == seq[0], src == seq[-1]),
                             [R(wt), R(src, c0, c1)], [R("ps", o, o + 512)])], acc=True)
                if src == seq[-1]:
                    cp(T.invz[:, c0:c1], T.ps[:, o:o + 512], [R("ps", o, o + 512)], [R("invz", c0, c1)], "vs"[b % 2])

        def rows(src, h, bank=4):
            c0, c1, o = h * H, (h + 1) * H, 512 * (bank + h)
            batch("t", [(lambda r=r: PE.matmul(T.ps[:, o:o + 64], T.dd[:, r * 128:(r + 1) * 128], T[src][:, c0 + r:c1:16], r == 0, r == 15),
                         [R("dd"), R(src, c0, c1)], [R("ps", o, o + 64)]) for r in range(16)], acc=True)

        def tab(lst, h, bank=4):
            o = 512 * (bank + h)
            ts(T[lst][:, h * 64:(h + 1) * 64], T.ps[:, o:o + 64], float(Z), None, OP.min, None, [R("ps", o, o + 64)], [R(lst, h * 64, (h + 1) * 64)])

        made = ["nl%d" % t for t in range(6)] + [None, "lm"]
        for t in range(8):
            w, old = ("na", "nb")[t % 2], ("nb", "na")[t % 2]
            src, ww, lst = ("invz", Z, "lb") if t == 0 else (old, WZ, made[t - 1] or "li")
            for h in range(2):
                if h == 1 and t > 0 and made[t - 1]:
                    tab(lst, 1)
                    give(lst, 1 if lst in EARLY else None)
                for e, c in (("v", h * H), ("s", h * H + 512)):
                    pick(e, w, c, src, 0, ww, lst, c // 16 + 128 * (t == 0), 512)
                if made[t]:
                    rows(w, h)
            if made[t]:
                tab(made[t], 0)
                if made[t] in EARLY:
                    give(made[t], 0)
            if WF and CFG["p_early"] < t <= 4:
                far_p(t - 1)
            if t == 2:
                for h in range(2):
                    rows("invz", h, 6)
            if t == 3:
                for h in range(2):
                    tab("li", h, 6)
                give("li")
        tab("lm", 1)
        give("lm")
        if CFG["fold"]:
            for i in range(len(TAIL)):
                round_down(i, 1, CFG["i1"][i], CFG["i2"][i])
                rest(i, 1)
        else:
            bank = [(T.ps[:, 512 * i:512 * i + c1 - c0], R("ps", 512 * i, 512 * i + 512)) for i, (c0, c1) in enumerate(TAIL)]
            ts(T.idf[:], T.i1[:], 0, None, OP.is_equal, None, [R("i1")], [R("idf")])
            ts(T.idh[:], T.i1[:], 0, None, OP.is_equal, None, [R("i1")], [R("idh")])
            fill("wa", 0.0)
            for i in CFG["self"]:
                last_step(i, "s")
                last_step(i, "v")
            for src in ("p1", "rfp", "raw"):
                for i in CFG["iorder"]:
                    c0, c1 = TAIL[i]
                    terms = ["p1"] + ["rfp"] * WF + ["raw"] * (CFG["i0"][i] == "t")
                    wt = "idh" if src == "rfp" else "idf"
                    if src in terms:
                        batch("t", [(lambda: PE.matmul(bank[i][0], T[wt][:], T[src][:, c0:c1], src == terms[0], src == terms[-1]),
                                     [R(wt), R(src, c0, c1)], [bank[i][1]])], acc=True)

            def step(i, n):
                c0, c1 = TAIL[i]
                if n == 0 and CFG["i0"][i] == "v":
                    tt(bank[i][0], bank[i][0], T.raw[:, c0:c1], OP.add, [bank[i][1], R("raw", c0, c1)], [bank[i][1]])
                elif n == 1:
                    affine(CFG["i1"][i], T.qq[:, c0:c1], bank[i][0], (1 + 2.0 ** -20) / 256, 2.0 ** 23 - 0.5, [bank[i][1]], [R("qq", c0, c1)])
                elif n == 2:
                    affine(CFG["i2"][i], T.pb[:, c0:c1], T.qq[:, c0:c1], -256.0, 2.0 ** 31, [R("qq", c0, c1)], [R("pb", c0, c1)])
                elif n == 3:
                    tt(T.yo[:, c0:c1], bank[i][0], T.pb[:, c0:c1], OP.add, [bank[i][1], R("pb", c0, c1)], [R("yo", c0, c1)])
                    store(c0, c1)
            lag = CFG["lag"]
            for i, n in sorted(((i, n) for i in range(len(TAIL)) for n in range(4)), key=lambda e: (e[0] + lag[e[1]], -e[1])):
                step(i, n)
    else:
        FQ = (fz, qsrc, "lfq", hasQ, 4)
        NP, NQ_ = (zone, "xs", "lnp", hasP, 0), (zone, qsrc, "lnq", hasQ, 4)
        plast = None if WF else "rfp"
        addup(*NP, [l], last=plast)
        if not QI:
            addup(*FQ, [l], range(3))
        choose()
        if not QI:
            addup(*FQ, [l], [3])
        if CFG["lb_first"]:
            send(C[rank + 1], "rpi", T.lb[:, 0:LW], T.lb[:, 0:LW], [R("lb")], on_es)
        near_x()
        if not CFG["lb_first"]:
            send(C[rank + 1], "rpi", T.lb[:, 0:LW], T.lb[:, 0:LW], [R("lb")], off_es)
        for z in picks:
            gather("s", z)
        order = arrival("lnq")
        for s in order:
            if at_w(s, l):
                cp(T.lq[:, s * 128:(s + 1) * 128], T.lpi[:, local[s] * 256 + zone // 2 * 128:local[s] * 256 + zone // 2 * 128 + 128], [R("lpi")], [R("lq", s * 128, (s + 1) * 128)])

        def pick_landed(e):
            for s in order:
                w = at_w(s, l) or ""
                for h in range(len(w)):
                    if w[h] == e:
                        n = Z // len(w)
                        pick(e, "lnq", s * Z + h * n, "lnp", s * Z, (s + 1) * Z, "lq", s * 128 + h * n // 16, n)
        pick_landed("s")
        for s in arrival("lnp")[:CFG["np_before"]]:
            addup(*NP, [s], last=plast)
        if not QI:
            add_landed(FQ, CFG["fqn"])
        if l in hasQ and nears[0] in picks:
            hand(nears[0], qsrc, "lnq")
        todo, pieces = list(mine), [i for i, f in enumerate(FAR) if f[0] == "q"]
        for n in () if QI else CFG["wweave"]:
            scat(todo[:n])
            if todo and not todo[n:]:
                send(C[rank + 1], "rinw", T.inw[:], T.inv[:], [R("inv")])
            todo = todo[n:]
            far_piece(pieces.pop(0))
        if todo:
            scat(todo)
            send(C[rank + 1], "rinw", T.inw[:], T.inv[:], [R("inv")])
        pick_landed("v")
        for n, s in enumerate(arrival("lnp")):
            if n == CFG["nq_own"]:
                addup(*NQ_, [l], last="rfq")
            if n >= CFG["np_before"]:
                addup(*NP, [s], last=plast)
        if CFG["nq_own"] == 3:
            addup(*NQ_, [l], last="rfq")
        for s in order[:CFG["nq_before"]]:
            addup(*NQ_, [s], last="rfq")
        for i, (kind, c0, c1, via) in sorted(enumerate(FAR), key=lambda e: e[1][3] is not None):
            if kind == "p" and not WF:
                addup(*NP, ["rfp"], range(c0 // 512, c1 // 512), "rfp")
        for b, e in ((1, "v"), (2, "s"), (3, "v"), (0, "s")):
            cp(T.p1[:, 512 * b:512 * b + 512], T.ps[:, 512 * b:512 * b + 512], [R("ps", 512 * b, 512 * b + 512)], [R("p1", 512 * b, 512 * b + 512)], e)
        for b, e in ((2, "v"), (3, "s"), (0, "v"), (1, "s")):
            pick(e, "pb", 512 * b, "p1", 0, Z, "lb", 32 * b, 512)
        for s in order[CFG["nq_before"]:]:
            addup(*NQ_, [s], last="rfq")
        for i in CFG["qorder"]:
            kind, c0, c1, via = [f for f in FAR if f[0] == "q"][i]
            if kind == "q":
                addup(*NQ_, ["rfq"], range(c0 // 512, c1 // 512), "rfq")
                for c in range(c0, c1, 512):
                    tt(T.wa[:, c:c + 512], T.ps[:, Z + c:Z + c + 512], T.pb[:, c:c + 512], OP.subtract,
                       [R("ps", Z + c, Z + c + 512), R("pb", c, c + 512)], [R("wa", c, c + 512)])
                    cp(T.vc[:, c:c + 512], T.wa[:, c:c + 512], [R("wa", c, c + 512)], [R("vc", c, c + 512)], "s")

        if not CFG["fold"]:
            send(C[rank + 1], "rp1", T.p1[:], T.p1[:], [R("p1")])
        for t in range(6):
            old, w = ("wa", "wb")[t % 2], ("wb", "wa")[t % 2]
            for c0, c1 in ((0, H), (H, Z)):
                comb(w, old, "nl%d" % t, "vc", c0, c1)
                if t < 5:
                    cp(T.vc[:, c0:c1], T[w][:, c0:c1], [R(w, c0, c1)], [R("vc", c0, c1)], "s")
                elif CFG["self"]:
                    send(C[rank + 1], "rwa%d" % (c0 // H), T.wa[:, c0:c1], T.wa[:, c0:c1], [R("wa", c0, c1)])
        for i in range(len(TAIL)):
            last_step(i, "s")
        for i, (c0, c1) in enumerate(TAIL):
            last_step(i, "v")
            if i in CFG["self"]:
                continue
            send_all([([rank + 1], "rz%d" % i, T.raw[:, c0:c1], [T.raw[:, c0:c1], T.p1[:, c0:c1]][:1 + CFG["fold"]], all_es)], [R("raw", c0, c1), R("p1", c0, c1)])
        for i in WFLOAT:
            round_down(i, -1)
        for i in range(len(TAIL)):
            if i not in WFLOAT:
                by_bits(i, -1)
        for i in WFLOAT:
            rest(i, -1)
    finish(sent[0])
